import numpy as np, ml_dtypes
CORES = [9,25,41,57]
N = 4
import mx_ref
BF = ml_dtypes.bfloat16
def f(rng, *shape):
    return mx_ref.flush((rng.standard_normal(shape, dtype=np.float32) * np.exp2(rng.integers(-2, 3, shape[:-1] + (1,)))).astype(BF))
def wide(rng, *shape, cols=0):
    v = rng.standard_normal(shape, dtype=np.float32) * np.exp2(rng.integers(-12, 13, shape)).astype(np.float32)
    if cols: v *= np.repeat(np.exp2(rng.integers(-cols, cols + 1, shape[:-2] + (1, shape[-1] // 4))) * (rng.random(shape[:-2] + (1, shape[-1] // 4)) > 0.0625), 4, axis=-1).astype(np.float32)
    return mx_ref.flush(v.astype(BF))
T, CAPP, O = 512, 192, 2
def scores(us, x):
    return mx_ref.matmul(mx_ref.quantize(us), mx_ref.quantize(x))[:8] + np.float32(0.0)
def winners(us, x):
    return np.argmax(np.stack([scores(us[s], x[s]) for s in range(N)]), axis=0)
def fill(rng, n, tot, most):
    n = np.array(n)
    while n.sum() < tot:
        q = rng.integers(0, N)
        if n[q] < most[q]: n[q] += 1
    return rng.permutation(np.repeat(np.arange(N), n))
def deal(rng, full):
    return np.stack([fill(rng, [CAPP if q in full[g] else 0 for q in range(N)], T, [CAPP] * N) for g in range(8)])
def one(rng):
    g, s = rng.integers(0, 8), rng.integers(0, N)
    return deal(rng, [[s] if i == g else [] for i in range(8)])
def heads(rng):
    u, h = np.zeros((8, 16, 128, 4), np.float32), np.arange(8)
    u[h, :, h] = rng.choice([-1.0, 1.0], (8, 16, 4)) * (0.25 + np.abs(rng.standard_normal((8, 16, 4)))) * np.exp2(rng.integers(-2, 3, (8, 16, 1)))
    return np.repeat(u.reshape(1, 128, 512).astype(BF), N, axis=0)
def plant(rng, x, us, wn, big=4, tie=None, zero=None):
    v = np.abs(x.astype(np.float32)).reshape(N, 8, 16, T, 4)
    v[v < 2.0 ** -24] = 0
    h, b = np.arange(8), np.float32(big)
    a = np.sign(us.astype(np.float32)).reshape(8, 16, 128, 4)[h, :, h][:, :, None]
    win = (wn == np.arange(N)[:, None, None])[:, :, None, :, None]
    neg = (rng.random((8, T)) < 0.125)[:, None, :, None]
    c = np.where(rng.random(v.shape, dtype=np.float32) < 0.5, np.float32(-1), np.float32(1))
    t = (np.where(neg, np.where(win, -a, -4 * b * a), np.where(win, b * a, c)) * v).astype(np.float32)
    s = np.stack([scores(us, t[r].reshape(128, 4 * T).astype(BF)) for r in range(N)])
    won = np.take_along_axis(s, wn[None], axis=0)[0]
    lost = np.where(win[:, :, 0, :, 0], -np.inf, s).max(axis=0)
    bad = (~(won - lost > 0.5 * np.abs(won)))[:, None, :, None]
    t = np.where(bad, np.where(win, b * a, -a) * v, t).astype(np.float32)
    if tie is not None:
        best = np.where(win, t, np.float32(0)).sum(axis=0)
        t = np.where(tie[:, None, :, None] & (wn < np.arange(N)[:, None, None])[:, :, None, :, None], best, t)
    if zero is not None: t[:, :, :, zero] = 0
    return t.reshape(N, 128, 4 * T).astype(BF)
def narrow(rng, x, us, wn):
    v, h = x.astype(np.float32).reshape(N, 8, 16, T, 4), np.arange(8)
    u = np.abs(us.astype(np.float32)).reshape(8, 16, 128, 4)[h, :, h]
    i, b = np.unravel_index(u.reshape(8, 64).argmin(axis=1), (16, 4))
    win = wn == np.arange(N)[:, None, None]
    part = np.where(win[:, :, None, :, None], v, np.float32(0)).sum(axis=0)
    p = np.exp2(np.floor(np.log2((u[:, :, None] * np.abs(part)).sum(axis=(1, 3))) - np.log2(u[h, i, b])[:, None]) - 12)
    z = np.stack([np.where(part[g, i[g], :, b[g]] < 0, -p[g], p[g]) for g in range(8)])
    close = np.repeat((rng.permutation(T) < T // 3)[None], 8, axis=0)
    other = (wn + rng.integers(1, N, (8, T))) % N
    hold = ((rng.random((N, 8, T)) < 0.25) | (other == np.arange(N)[:, None, None])) & ~win & close
    held = hold | (win & close)
    t = np.where(held[:, :, None, :, None], part, v).astype(np.float32)
    d = np.where(hold, rng.choice([-0.125, 0.125], (N, 8, T)), 0.0)
    for k in range(2):
        for g in range(8): t[:, g, i[g], :, b[g]] = np.where(held[:, g], z[g] * (1.5 + d[:, g]), t[:, g, i[g], :, b[g]])
        s = np.stack([scores(us, t[r].reshape(128, 4 * T).astype(BF)) for r in range(N)])
        if k == 0: d = np.where(s == np.take_along_axis(s, wn[None], axis=0), 2 * d, d)
    now = np.argmax(s, axis=0)
    for g in range(8):
        for k in range(T):
            n = np.bincount(now[g], minlength=N)
            q = n.argmax()
            if n[q] <= CAPP: break
            j = rng.permutation(np.flatnonzero((now[g] == q) & (wn[g] != q)))[:n[q] - CAPP]
            now[g, j] = wn[g, j]; close[g, j] = False
    return np.where(close[:, None, :, None], t, v).reshape(N, 128, 4 * T).astype(BF)
def draw(rng, wn, **k):
    us = heads(rng)
    return {"x": plant(rng, f(rng, N, 128, 4 * T), us[0], wn, **k), "us": us, "w": f(rng, N, 128, 512 * O)}
def setup_inputs(rng):
    return draw(rng, one(rng))
def setup_inputs_equal(rng):
    e, p = CAPP - 8, rng.permutation(T)
    far = np.stack([fill(rng, [8] + [0] * (N - 1), T - e, [8] + [CAPP] * (N - 1)) for g in range(8)])
    wn = np.concatenate([np.zeros((8, e), int), far], axis=1)[:, p]
    tie = np.repeat(np.concatenate([np.ones(e, bool), np.arange(T - e) % 2 == 0])[None], 8, axis=0)[:, p]
    return draw(rng, wn, tie=tie, zero=(np.arange(T) < 4)[p])
def setup_inputs_full(rng):
    s, k = int(rng.integers(0, N)), T // CAPP
    return draw(rng, deal(rng, [[s] + [q for q in rng.permutation(N).tolist() if q != s][:k - 1] for g in range(8)]))
def setup_inputs_near(rng):
    wn = one(rng)
    d = draw(rng, wn); d["x"] = narrow(rng, d["x"], d["us"][0], wn); return d
def setup_inputs_spread(rng):
    wn, us = one(rng), heads(rng)
    e = np.exp2(rng.integers(-4, 5, (N, 8, 1, T, 1))) * ((rng.random((N, 8, 1, T, 1)) > 0.0625) | (wn == np.arange(N)[:, None, None])[:, :, None, :, None])
    x = wide(rng, N, 128, 4 * T).astype(np.float32).reshape(N, 8, 16, T, 4) * e.astype(np.float32)
    return {"x": plant(rng, x, us[0], wn, big=256), "us": us, "w": f(rng, N, 128, 512 * O)}
def setup_inputs_stretch(rng):
    L = []
    for g in range(8):
        s, a = rng.integers(0, N), rng.choice([0, T - CAPP, rng.integers(0, T - CAPP + 1)])
        far = fill(rng, [0] * N, T - CAPP, [0 if q == s else CAPP for q in range(N)])
        L.append(np.concatenate([far[:a], np.full(CAPP, s), far[a:]]))
    return draw(rng, np.stack(L))
def check_inputs(d):
    b = []
    for k in ("x", "us", "w"):
        v = np.abs(np.asarray(d[k]).astype(np.float32))
        if not ((v == 0) | ((v >= 2.0 ** -30) & (v <= 2.0 ** 30))).all(): b.append(k)
    if b: return b
    u, h = np.array(d["us"]).astype(np.float32), np.arange(8)
    same = (u == u[:1]).all()
    u = u.reshape(N, 8, 16, 128, 4); u[:, h, :, h] = 0
    if not same or (u != 0).any(): b.append("us")
    wn = winners(d["us"], d["x"])
    if max((wn == s).sum(axis=1).max() for s in range(N)) > CAPP: b.append("x")
    return b
def reference(x, us, w):
    wn = winners(us, x)
    M = []
    for s in range(N):
        v = np.where((wn == s)[:, None, :, None], x[s].astype(np.float32).reshape(8, 16, T, 4), np.float32(0))
        M.append(mx_ref.quantize(np.ascontiguousarray(v.reshape(128, 4 * T).astype(BF))))
    y = np.zeros((N, 128, O * T), np.float32)
    for r in range(N):
        for o in range(O):
            W = mx_ref.quantize(np.ascontiguousarray(w[r][:, 512 * o:512 * o + 512]))
            for s in range(N): y[r][:, T * o:T * o + T] += mx_ref.matmul(W, M[s])
    return {"y": y, "wn": np.repeat(wn.astype(np.float32)[None], N, axis=0)}

@@ -1,0 +1,311 @@
+from concourse.bass import DstId, RemoteDMATransfer
+from concourse.mybir import dt, AluOpType, ActivationFunctionType
+
+CAP = 192
+NR = 4
+RW = NR * CAP
+LW = 1136
+F, I32, U16, BF, X4, U8 = "float32", "int32", "uint16", "bfloat16", "float8_e4m3fn_x4", "uint8"
+_sb = {
+    "us_sb": (32, BF), "ut": (4 * 288, BF), "uq": (288, X4), "up": (288, U8),
+    "xb": (4 * 608, BF), "xq": (608, X4), "xp": (608, U8),
+    "zt": (512, BF), "wm": (8192, BF), "wq": (2048, X4), "wp": (2048, U8),
+    "cb": (4 * CAP, BF), "lq": (RW, X4), "lp": (RW, U8), "sc": (128, F),
+    "ip": (1, I32), "i15": (1, I32), "ial": (1, I32), "it3": (1, I32), "alf": (1, F), "t3f": (1, F), "a32": (1, F),
+    "vi": (512, F), "vv": (512, F), "bi": (32, F), "dl": (32, F), "dc": (32, F), "ki": (240, F), "k1": (240, F), "k2": (240, F),
+    "kk": (240, F), "mi": (128, F), "m16": (128, F), "ni": (128, F), "m32": (128, F),
+    "mx1": (32, F), "mx2": (32, F), "cl1": (32, F), "cl2": (32, F), "win": (32, F), "ra": (32, F), "rt": (64, F), "ea": (32, F),
+    "et": (32, F), "w2": (32, F), "u2": (32, F), "ta": (32, F), "oi": (32, I32), "ou": (32, U16), "ll": (LW, F), "sl5": (240, F),
+    "offa": (48, U16),
+    "m64": (64, F), "mm": (32, F), "ne": (96, F), "q2": (32, F), "q1": (32, F), "q0": (32, F), "wnt": (32, F), "ww": (128, F),
+    "rr": (128, F), "rt4": (160, F), "e4": (128, F), "et4": (128, F), "p4": (128, F), "pm": (128, F), "ph": (64, F), "pi": (32, F),
+    "ptr": (32, F), "zz": (256, F), "offb": (256, U16),
+    "rw": (16 * RW, F), "g0": (512, F), "g1": (512, F), "g5": (512, F), "g6": (512, F), "ac0": (512, F), "ac1": (512, F),
+    "ac2": (512, F), "ac3": (512, F),
+}
+SCRATCH = {k: ("sbuf", [128, n], d) for k, (n, d) in _sb.items()}
+SCRATCH["d2"] = ("dram", [16, 256], F)
+for _k in range(8):
+    SCRATCH["ps%d" % _k] = ("psum", [128, 512], F)
+SEMAPHORES = (["v", "a", "pv", "pa", "px", "gi", "us", "wn", "d2s", "zs", "ga", "y0", "y1", "y2", "sloc", "cloc"]
+              + ["x%d" % i for i in range(4)] + ["w%d" % i for i in range(4)]
+              + ["s%d" % i for i in range(4)] + ["c%d" % i for i in range(4)])
+
+
+def rank_program(g, core, T, topo):
+    r = T.rank_of(core)
+    if r is None:
+        return
+    A = AluOpType
+    COPY = ActivationFunctionType.Copy
+    IDENT = ActivationFunctionType.Identity
+    Q = {"g": g, "v": g.vector, "a": g.scalar, "p": g.tensor, "s": g.sync}
+    seen = {k: {} for k in Q}
+    cnt = {}
+
+    def need(qn, deps):
+        for s, n in deps:
+            if seen[qn].get(s, 0) < n:
+                Q[qn].wait_ge(T.sem[s], n)
+                seen[qn][s] = n
+
+    def op(qn, deps, call, sem, n=1):
+        need(qn, deps)
+        call().then_inc(T.sem[sem], n)
+        cnt[sem] = cnt.get(sem, 0) + n
+        return (sem, cnt[sem])
+
+    V = g.vector
+    S = g.scalar
+
+    def v(deps, call):
+        return op("v", deps, call, "v")
+
+    def a(deps, call):
+        return op("a", deps, call, "a")
+
+    def dma(qn, deps, out, in_, sem):
+        return op(qn, deps, lambda: Q[qn].dma_start(out, in_), sem, 16)
+
+    peers = [(r + k) % NR for k in (1, 2, 3)]
+    senders = [(r - k) % NR for k in (1, 2, 3)]
+
+    t_us = dma("s", [], T.us_sb[:], T.us[:, 0:32], "us")
+    t_x = {}
+    for i, qn in ((3, "s"), (2, "a"), (1, "s"), (0, "a")):
+        t_x[i] = dma(qn, [], T.xb[:, 512 * i:512 * i + 512], T.x[:, 512 * i:512 * i + 512], "x%d" % i)
+
+    def io(out, pattern, base, cm):
+        return op("g", [], lambda: g.iota(out, pattern, base, cm, allow_small_or_imprecise_dtypes=True), "gi")
+    io(T.ip[:], [[0, 1]], 0, 1)
+    io(T.bi[:], [[1, 32]], 200, 0)
+    io(T.ki[:], [[0, 48], [1, 5]], 0, 0)
+    io(T.mi[:], [[0, 8], [1, 16]], 0, 0)
+    t_small = io(T.ni[:], [[0, 4], [1, 32]], 0, 0)
+    t_vi = io(T.vi[:], [[4, 32], [128, 16]], 0, 0)
+
+    t_zt = v([], lambda: V.memset(T.zt[:], 0.0))
+    v([], lambda: V.memset(T.ut[:], 0.0))
+    v([], lambda: V.memset(T.xb[:, 2048:2432], 0.0))
+    v([], lambda: V.memset(T.ll[:, 0:240], 2048.0))
+    v([], lambda: V.memset(T.rt[:, 0:32], 0.0))
+    t_f = v([], lambda: V.memset(T.rt4[:, 0:32], 0.0))
+    t_z = {}
+    for h in range(3):
+        t_z[h] = v([], lambda: V.memset(T.wm[:, 1024 * h:1024 * h + 1024], 0.0))
+    for h in range(3, 8):
+        for k in range(2):
+            c0 = 1024 * h + 512 * k
+            t_z[h] = a([t_zt], lambda: S.activation(T.wm[:, c0:c0 + 512], T.zt[:], COPY))
+
+    t_w = {}
+    for h in range(8):
+        t_w[h // 2] = dma("s", [t_z[h]], T.wm[16 * h:16 * h + 16, 1024 * h:1024 * h + 1024], T.w[16 * h:16 * h + 16, :],
+                          "w%d" % (h // 2))
+
+    for base in (4 * 15, 4 * (144 + 16)):
+        for e in range(4):
+            t_ut = v([t_us, t_f], lambda: V.tensor_copy(T.ut[:, base + e:base + e + 449:64], T.us_sb[:, e:32:4]))
+    t_uq = v([t_ut], lambda: V.quantize_mx(T.uq[:], T.up[:], T.ut[:]))
+    for i in (3, 2, 1, 0):
+        lo, hi = 128 * i, (608 if i == 3 else 128 * i + 128)
+        t_q = v([t_x[i]], lambda: V.quantize_mx(T.xq[:, lo:hi], T.xp[:, lo:hi], T.xb[:, 4 * lo:4 * hi]))
+        need("p", [t_uq, t_q])
+        for k in (4 * i + 3, 4 * i + 2, 4 * i + 1, 4 * i):
+            st = 15 - k if k % 2 else 144 + 16 - k
+            call = lambda: g.tensor.matmul_mx(T.ps0[:, 0:128], T.uq[:, st:st + 128], T.up[:, st:st + 128],
+                                              T.xq[:, 32 * k:32 * k + 128], T.xp[:, 32 * k:32 * k + 128], k == 15, k == 0)
+            if k:
+                call()
+            else:
+                t_sm = op("p", [], call, "px")
+    t_own = v([t_sm], lambda: V.tensor_copy(T.sc[:, 32 * r:32 * r + 32], T.ps0[:, 0:32]))
+
+    def send(dst, view, rsem, lsem):
+        d = T.cores[dst]
+        rid, pid, _se = topo.addr(d)
+        g.remote_dma(view, view, T.sem[rsem], T.sem[lsem], pid, rid, topo.mask(core, d))
+        cnt[lsem] = cnt.get(lsem, 0) + len(topo.engines(core, d))
+
+    def send_all(view, rsem, lsem):
+        ds = [T.cores[d] for d in peers]
+        ids = [DstId(rid=topo.addr(d)[0], pnc=topo.addr(d)[1]) for d in ds]
+        g.remote_dma_fused([RemoteDMATransfer(dst_ids=ids, dma_engine_mask=topo.mask(core, ds[0]), remote_sem=T.sem[rsem],
+                                              srcs=[view], dsts=[view] * 3)], local_sem=T.sem[lsem])
+        cnt[lsem] = cnt.get(lsem, 0) + len(topo.engines(core, ds[0]))
+
+    need("g", [t_own])
+    send_all(T.sc[:, 32 * r:32 * r + 32], "s%d" % r, "sloc")
+    n_in = {s: len(topo.engines(T.cores[s], core)) for s in senders}
+
+    c1 = v([t_small], lambda: V.tensor_scalar(T.i15[:], T.ip[:], 15, None, A.bitwise_and))
+    c2 = v([], lambda: V.tensor_scalar(T.ial[:], T.ip[:], 15, 2, A.bitwise_and, A.arith_shift_right))
+    c3 = v([], lambda: V.tensor_scalar(T.it3[:], T.ip[:], 3, None, A.bitwise_and))
+    v([], lambda: V.tensor_scalar(T.m16[:], T.mi[:], 0.5, None, A.is_gt))
+    v([], lambda: V.tensor_scalar(T.m32[:], T.ni[:], 0.5, None, A.is_gt))
+    c4 = v([], lambda: V.tensor_scalar(T.k2[:], T.ki[:], 4.0, 4096.0, A.is_equal, A.mult))
+    c5 = v([c1], lambda: V.tensor_scalar(T.a32[:], T.i15[:], 32.0, None, A.mult))
+    c6 = v([c2], lambda: V.tensor_copy(T.alf[:], T.ial[:]))
+    c7 = v([c3], lambda: V.tensor_copy(T.t3f[:], T.it3[:]))
+    v([c5], lambda: V.tensor_scalar(T.dl[:], T.bi[:], T.a32[:], None, A.add))
+    v([], lambda: V.tensor_scalar(T.dc[:], T.bi[:], T.a32[:], -1.3, A.add, A.add))
+    c8 = v([c6], lambda: V.tensor_scalar(T.k1[:], T.ki[:], T.alf[:], 4096.0, A.is_lt, A.mult))
+    t_const = v([c4, c8], lambda: V.tensor_tensor(T.kk[:], T.k1[:], T.k2[:], A.max))
+    t_vv = a([c7, t_vi], lambda: S.activation(T.vv[:], T.vi[:], IDENT, bias=T.t3f[:]))
+
+    def quant_w(i):
+        return v([t_w[i]], lambda: V.quantize_mx(T.wq[:, 512 * i:512 * i + 512], T.wp[:, 512 * i:512 * i + 512],
+                                                 T.wm[:, 2048 * i:2048 * i + 2048]))
+    for i in range(3):
+        t_wq = quant_w(i)
+
+    def score(s):
+        return T.sc[:, 32 * s:32 * s + 32]
+
+    def arrived(s):
+        return [("s%d" % s, n_in[s])]
+    conds = []
+    for side, buf, cbuf, cmp in ((lambda s: s < r, T.mx1, T.cl1, A.is_gt), (lambda s: s > r, T.mx2, T.cl2, A.is_ge)):
+        grp = [s for s in senders if side(s)]
+        if not grp:
+            continue
+        cur, tk = score(grp[0]), []
+        need("v", arrived(grp[0]))
+        for n, s in enumerate(grp[1:]):
+            nxt = buf[:] if n == 0 else T.win[:]
+            tk = [v(tk + arrived(s), lambda: V.tensor_tensor(nxt, cur, score(s), A.max))]
+            cur = nxt
+        conds.append((cbuf, v(tk + [t_own], lambda: V.tensor_tensor(cbuf[:], score(r), cur, cmp))))
+    if len(conds) == 2:
+        wn_ = T.win
+        t_win = v([conds[0][1], conds[1][1]], lambda: V.tensor_tensor(T.win[:], T.cl1[:], T.cl2[:], A.mult))
+    else:
+        wn_, t_win = conds[0]
+    m16a, m32a = T.m16[:, 0:32], T.m32[:, 0:32]
+    t1 = v([t_win, t_const], lambda: V.tensor_tensor_scan(T.ra[:], m32a, wn_[:], 0.0, A.mult, A.add))
+    b1 = v([], lambda: V.tensor_tensor(T.w2[:], wn_[:], T.dl[:], A.mult))
+    t2 = v([t1], lambda: V.transpose(T.rt[:, 32:64], T.ra[:]))
+    b2 = v([b1], lambda: V.tensor_tensor(T.u2[:], T.dc[:], T.w2[:], A.subtract))
+    t3 = v([t2], lambda: V.tensor_tensor_scan(T.ea[:], T.rt[:, 31:63], m16a, 0.0, A.add, A.mult))
+    b3 = v([b2], lambda: V.tensor_tensor(T.ta[:], T.u2[:], T.ra[:], A.add))
+    t4 = v([t3], lambda: V.transpose(T.et[:], T.ea[:]))
+    m1 = v([], lambda: V.tensor_tensor(T.m64[:], T.sc[:, 0:64], T.sc[:, 64:128], A.max))
+    t5 = v([t4, b3], lambda: V.tensor_scalar(T.oi[:], T.ta[:], T.et[:, 31:32], 1.25, A.add, A.mult))
+    m2 = v([m1], lambda: V.tensor_tensor(T.mm[:], T.m64[:, 0:32], T.m64[:, 32:64], A.max))
+    t6 = v([t5], lambda: V.tensor_copy(T.ou[:], T.oi[:]))
+    n2 = v([m2], lambda: V.tensor_tensor(T.ne[:, 64:96], score(2), T.mm[:], A.not_equal))
+    t7 = v([t6, t_vv], lambda: V.tensor_copy(T.ll[:].indirect(T.ou[:]), T.vv[:]))
+    n1 = v([], lambda: V.tensor_tensor(T.ne[:, 32:64], score(1), T.mm[:], A.not_equal))
+    t8 = v([t7], lambda: V.tensor_tensor_scan(T.sl5[:], T.ll[:, 0:240], T.kk[:], 4096.0, A.min, A.max))
+    n0 = v([], lambda: V.tensor_tensor(T.ne[:, 0:32], score(0), T.mm[:], A.not_equal))
+    t9 = v([t8], lambda: V.tensor_copy(T.offa[:], T.sl5[:, 3:240:5]))
+    q2 = v([n2], lambda: V.tensor_scalar(T.q2[:], T.ne[:, 64:96], 1.0, None, A.add))
+    t10 = a([t9], lambda: S.activation(T.cb[:, 384:768], T.xb[:].indirect(T.offa[:, 24:48]), COPY))
+    t11 = v([t9], lambda: V.tensor_copy(T.cb[:, 0:384], T.xb[:].indirect(T.offa[:, 0:24])))
+    q1 = v([q2, n1], lambda: V.tensor_tensor(T.q1[:], T.ne[:, 32:64], T.q2[:], A.mult))
+    lo = CAP * r
+    t_c = v([t10, t11], lambda: V.quantize_mx(T.lq[:, lo:lo + CAP], T.lp[:, lo:lo + CAP], T.cb[:]))
+    need("g", [t_c])
+    for d in peers:
+        send(d, T.lq[:, lo:lo + CAP].bitcast(dt.uint8), "c%d" % r, "cloc")
+        send(d, T.lp[:, lo:lo + CAP], "c%d" % r, "cloc")
+    t_wq3 = quant_w(3)
+
+    t = v([q1], lambda: V.tensor_scalar(T.q0[:], T.q1[:], 1.0, None, A.add))
+    t_wn = v([t, n0], lambda: V.tensor_tensor(T.wnt[:], T.ne[:, 0:32], T.q0[:], A.mult))
+    for s in range(NR):
+        t = v([t_wn], lambda: V.tensor_scalar(T.ww[:, 32 * s:32 * s + 32], T.wnt[:], float(s), None, A.is_equal))
+    t = v([t], lambda: V.tensor_tensor_scan(T.rr[:], T.m32[:], T.ww[:], 0.0, A.mult, A.add))
+    t = v([t], lambda: V.transpose(T.rt4[:, 32:160], T.rr[:]))
+    t = v([t], lambda: V.tensor_tensor_scan(T.e4[:], T.rt4[:, 31:159], T.m16[:], 0.0, A.add, A.mult))
+    t = v([t], lambda: V.transpose(T.et4[:], T.e4[:]))
+    for s in range(NR):
+        c = 32 * s
+        tp = v([t], lambda: V.tensor_scalar(T.p4[:, c:c + 32], T.rr[:, c:c + 32], T.et4[:, c + 31:c + 32],
+                                            float(CAP * s - 1), A.add, A.add))
+    t = v([tp], lambda: V.tensor_tensor(T.pm[:], T.p4[:], T.ww[:], A.mult))
+    t = v([t], lambda: V.tensor_tensor(T.ph[:], T.pm[:, 0:64], T.pm[:, 64:128], A.add))
+    t = v([t], lambda: V.tensor_tensor(T.pi[:], T.ph[:, 0:32], T.ph[:, 32:64], A.add))
+    t_pt = v([t], lambda: V.transpose(T.ptr[:], T.pi[:]))
+    for ab in range(4):
+        for bh in range(2):
+            p0, c0 = 32 * ab + 16 * bh, 128 * bh + 32 * ab
+            t_d2 = dma("s", [t_pt], T.d2[0:16, c0:c0 + 32], T.ptr[p0:p0 + 16, :], "d2s")
+    for k in range(8):
+        t_zz = dma("s", [t_d2], T.zz[16 * k:16 * k + 16, :], T.d2[:], "zs")
+    dma("s", [t_wn], T.wn[:], T.wnt[:], "wn")
+
+    banks = {"v": [T.ps0, T.ps1, T.ps2, T.ps3], "a": [T.ps4, T.ps5, T.ps6, T.ps7]}
+    hist = {"v": [], "a": []}
+    ready = {}
+
+    def product(s, h, o, e, deps):
+        n = len(hist[e])
+        bank = banks[e][n % 4]
+        old = [hist[e][n - 4]] if n >= 4 else [t_own]
+        w0, c0 = 256 * h + 128 * o, CAP * s
+        tk = op("p", deps + old + [t_wq if h < 6 else t_wq3], lambda: g.tensor.matmul_mx(
+            bank[:, 0:CAP], T.wq[:, w0:w0 + 128], T.wp[:, w0:w0 + 128], T.lq[:, c0:c0 + CAP], T.lp[:, c0:c0 + CAP],
+            True, True), "p" + e)
+        d0 = RW * (2 * h + o) + c0
+        if e == "v":
+            c = v([tk], lambda: V.tensor_copy(T.rw[:, d0:d0 + CAP], bank[:, 0:CAP]))
+        else:
+            c = a([tk], lambda: S.activation(T.rw[:, d0:d0 + CAP], bank[:, 0:CAP], COPY))
+        hist[e].append(c)
+        ready[(s, h, o)] = c
+
+    def window(h, o):
+        d0 = RW * (2 * h + o)
+        return T.rw[:, d0:d0 + RW]
+
+    def rdeps(h, o):
+        return [ready[(s, h, o)] for s in range(NR)]
+
+    jobs = [(h, o) for h in range(8) for o in range(2)]
+    for n, (h, o) in enumerate(jobs):
+        product(r, h, o, "v" if n % 4 == 3 else "a", [t_c])
+    for s in senders[:2]:
+        for n, (h, o) in enumerate(jobs):
+            product(s, h, o, "v" if n % 2 else "a", [("c%d" % s, 2 * n_in[s])])
+    for bh in range(2):
+        t_ob = v([t_zz], lambda: V.tensor_copy(T.offb[:, bh:256:2], T.zz[:, 128 * bh:128 * bh + 128]))
+    s = senders[2]
+    dep = [("c%d" % s, 2 * n_in[s])]
+
+    def gath(out, h, o):
+        return a(rdeps(h, o) + [t_ob], lambda: S.activation(out[:], window(h, o).indirect(T.offb[:, 32 * h:32 * h + 32]), COPY))
+    for h, o, e in ((7, 0, "a"), (0, 0, "v"), (1, 0, "v")):
+        product(s, h, o, e, dep)
+    t_g0 = gath(T.g0, 7, 0)
+    for h, o, e in ((5, 0, "a"), (2, 0, "v"), (3, 0, "v"), (6, 0, "a"), (4, 0, "v"), (0, 1, "v"), (1, 1, "v")):
+        product(s, h, o, e, dep)
+    t_g5 = gath(T.g5, 5, 0)
+    t_g6 = gath(T.g6, 6, 0)
+    t_ga = op("g", [t_g5, t_g6], lambda: g.dma_start(T.g6[:], T.g5[:], accum_op=A.add), "ga", 16)
+    product(s, 7, 1, "a", dep)
+    t_g1 = gath(T.g1, 7, 1)
+    for h in (2, 3, 4, 5, 6):
+        product(s, h, 1, "a", dep)
+
+    cur, tk = T.g0, [t_g0]
+    for h in range(5):
+        out = (T.ac0, T.ac1)[h % 2]
+        tk = [v(tk + rdeps(h, 0) + [t_ob], lambda: V.tensor_tensor(
+            out[:], window(h, 0).indirect(T.offb[:, 32 * h:32 * h + 32]), cur[:], A.add))]
+        cur = out
+    t_y0 = dma("s", tk, T.y[:, 0:512], cur[:], "y0")
+    op("g", [t_ga, t_y0], lambda: g.dma_start(T.y[:, 0:512], T.g6[:], accum_op=A.add), "ga", 16)
+    cur, tk = T.g1, [t_g1]
+    for h in range(6):
+        out = (T.ac2, T.ac3)[h % 2]
+        tk = [v(tk + rdeps(h, 1), lambda: V.tensor_tensor(
+            out[:], window(h, 1).indirect(T.offb[:, 32 * h:32 * h + 32]), cur[:], A.add))]
+        cur = out
+    for k in range(2):
+        c0 = 256 * k
+        t_l = v(tk + rdeps(6, 1), lambda: V.tensor_tensor(
+            T.ac2[:, c0:c0 + 256], window(6, 1).indirect(T.offb[:, 192 + 16 * k:192 + 16 * k + 16]), cur[:, c0:c0 + 256], A.add))
+        dma(("s", "a")[k], [t_l], T.y[:, 512 + c0:768 + c0], T.ac2[:, c0:c0 + 256], "y%d" % (1 + k))
+
+    need("g", sorted(cnt.items()))

@@ -4,30 +4,27 @@ from concourse.mybir import dt, AluOpType, ActivationFunctionType
 CAP = 192
 NR = 4
 RW = NR * CAP
-LW = 1136
+LW = 5632
+SLOT = (0, 2, 1, 3)
 F, I32, U16, BF, X4, U8 = "float32", "int32", "uint16", "bfloat16", "float8_e4m3fn_x4", "uint8"
 _sb = {
     "us_sb": (32, BF), "ut": (4 * 288, BF), "uq": (288, X4), "up": (288, U8),
     "xb": (4 * 608, BF), "xq": (608, X4), "xp": (608, U8),
     "zt": (512, BF), "wm": (8192, BF), "wq": (2048, X4), "wp": (2048, U8),
     "cb": (4 * CAP, BF), "lq": (RW, X4), "lp": (RW, U8), "sc": (128, F),
-    "ip": (1, I32), "i15": (1, I32), "ial": (1, I32), "it3": (1, I32), "alf": (1, F), "t3f": (1, F), "a32": (1, F),
-    "vi": (512, F), "vv": (512, F), "bi": (32, F), "dl": (32, F), "dc": (32, F), "ki": (240, F), "k1": (240, F), "k2": (240, F),
-    "kk": (240, F), "mi": (128, F), "m16": (128, F), "ni": (128, F), "m32": (128, F),
-    "mx1": (32, F), "mx2": (32, F), "cl1": (32, F), "cl2": (32, F), "win": (32, F), "ra": (32, F), "rt": (64, F), "ea": (32, F),
-    "et": (32, F), "w2": (32, F), "u2": (32, F), "ta": (32, F), "oi": (32, I32), "ou": (32, U16), "ll": (LW, F), "sl5": (240, F),
-    "offa": (48, U16),
-    "m64": (64, F), "mm": (32, F), "ne": (96, F), "q2": (32, F), "q1": (32, F), "q0": (32, F), "wnt": (32, F), "ww": (128, F),
-    "rr": (128, F), "rt4": (160, F), "e4": (128, F), "et4": (128, F), "p4": (128, F), "pm": (128, F), "ph": (64, F), "pi": (32, F),
-    "ptr": (32, F), "zz": (256, F), "offb": (256, U16),
-    "rw": (16 * RW, F), "g0": (512, F), "g1": (512, F), "g5": (512, F), "g6": (512, F), "ac0": (512, F), "ac1": (512, F),
-    "ac2": (512, F), "ac3": (512, F),
+    "ip": (1, I32), "ial": (1, I32), "it3": (1, I32), "alf": (1, F), "t3f": (1, F),
+    "vi": (512, F), "dl": (32, F), "dc": (32, F), "ki": (240, F), "kk": (240, F), "one": (128, F), "m32": (128, F), "lim": (32, F),
+    "ab": (64, F), "m64": (64, F), "cc": (64, F), "ww": (128, F), "rr": (1024, F), "rt": (64, F), "ea": (32, F), "et": (32, F),
+    "w2": (32, F), "u2": (32, F), "ta": (32, F), "oi": (32, I32), "ou": (32, U16), "ll": (LW, F), "sl5": (240, F), "offa": (48, U16),
+    "p4": (128, F), "pm": (128, F), "ph": (64, F), "dd": (64, F), "xf": (64, F), "xu": (64, U16), "offb": (256, U16),
+    "q1": (32, F), "q2": (32, F), "wnt": (32, F),
+    "rw": (16 * RW, F), "g0": (512, F), "g1": (512, F), "g4": (512, F), "g5": (512, F), "g6": (512, F), "ac0": (512, F),
+    "ac1": (512, F), "ac2": (512, F), "ac3": (512, F),
 }
 SCRATCH = {k: ("sbuf", [128, n], d) for k, (n, d) in _sb.items()}
-SCRATCH["d2"] = ("dram", [16, 256], F)
 for _k in range(8):
     SCRATCH["ps%d" % _k] = ("psum", [128, 512], F)
-SEMAPHORES = (["v", "a", "pv", "pa", "px", "gi", "us", "wn", "d2s", "zs", "ga", "y0", "y1", "y2", "sloc", "cloc"]
+SEMAPHORES = (["v", "a", "pv", "pa", "px", "gi", "us", "wn", "ob0", "ob1", "ob2", "ob3", "ga", "gb", "gc_", "y0", "y1", "y2", "sloc", "cloc"]
               + ["x%d" % i for i in range(4)] + ["w%d" % i for i in range(4)]
               + ["s%d" % i for i in range(4)] + ["c%d" % i for i in range(4)])
 
@@ -69,47 +66,53 @@ def rank_program(g, core, T, topo):
 
     peers = [(r + k) % NR for k in (1, 2, 3)]
     senders = [(r - k) % NR for k in (1, 2, 3)]
+    u = SLOT[r]
 
     t_us = dma("s", [], T.us_sb[:], T.us[:, 0:32], "us")
     t_x = {}
-    for i, qn in ((3, "s"), (2, "a"), (1, "s"), (0, "a")):
+    for i, qn in ((3, "a"), (2, "s"), (1, "a"), (0, "s")):
         t_x[i] = dma(qn, [], T.xb[:, 512 * i:512 * i + 512], T.x[:, 512 * i:512 * i + 512], "x%d" % i)
 
     def io(out, pattern, base, cm):
-        return op("g", [], lambda: g.iota(out, pattern, base, cm, allow_small_or_imprecise_dtypes=True), "gi")
-    io(T.ip[:], [[0, 1]], 0, 1)
-    io(T.bi[:], [[1, 32]], 200, 0)
-    io(T.ki[:], [[0, 48], [1, 5]], 0, 0)
-    io(T.mi[:], [[0, 8], [1, 16]], 0, 0)
-    t_small = io(T.ni[:], [[0, 4], [1, 32]], 0, 0)
-    t_vi = io(T.vi[:], [[4, 32], [128, 16]], 0, 0)
+        return op("g", [("gi", cnt.get("gi", 0))], lambda: g.iota(out, pattern, base, cm, allow_small_or_imprecise_dtypes=True), "gi")
+    t_ip = io(T.ip[:], [[0, 1]], 0, 1)
+    t_ki = io(T.ki[:], [[0, 48], [1, 5]], -1, 0)
+    t_dl = io(T.dl[:], [[1, 32]], 200, 32)
+    t_one = io(T.one[:], [[0, 128]], 1, 0)
+    for b in range(4):
+        io(T.lim[32 * b:32 * b + 32, :], [[0, 2], [4096, 16]], -1, CAP)
+    op("g", [("gi", cnt["gi"])], lambda: g.affine_select(T.m32[:], T.one[:], [[0, 4], [1, 32]], A.is_gt, 0.0, 0, 0), "gi")
+    t_gc = io(T.vi[:], [[4, 32], [128, 16]], 0, 0)
 
     t_zt = v([], lambda: V.memset(T.zt[:], 0.0))
-    v([], lambda: V.memset(T.ut[:], 0.0))
-    v([], lambda: V.memset(T.xb[:, 2048:2432], 0.0))
-    v([], lambda: V.memset(T.ll[:, 0:240], 2048.0))
-    v([], lambda: V.memset(T.rt[:, 0:32], 0.0))
-    t_f = v([], lambda: V.memset(T.rt4[:, 0:32], 0.0))
+    t_u0 = v([], lambda: V.memset(T.ut[:], 0.0))
+    t_f = v([], lambda: V.memset(T.xb[:, 2048:2432], 0.0))
     t_z = {}
-    for h in range(3):
-        t_z[h] = v([], lambda: V.memset(T.wm[:, 1024 * h:1024 * h + 1024], 0.0))
-    for h in range(3, 8):
-        for k in range(2):
-            c0 = 1024 * h + 512 * k
-            t_z[h] = a([t_zt], lambda: S.activation(T.wm[:, c0:c0 + 512], T.zt[:], COPY))
 
-    t_w = {}
-    for h in range(8):
-        t_w[h // 2] = dma("s", [t_z[h]], T.wm[16 * h:16 * h + 16, 1024 * h:1024 * h + 1024], T.w[16 * h:16 * h + 16, :],
-                          "w%d" % (h // 2))
+    def zero_a(h, k):
+        c0 = 1024 * h + 512 * k
+        t_z[h] = a([t_zt], lambda: S.activation(T.wm[:, c0:c0 + 512], T.zt[:], COPY))
 
-    for base in (4 * 15, 4 * (144 + 16)):
-        for e in range(4):
-            t_ut = v([t_us, t_f], lambda: V.tensor_copy(T.ut[:, base + e:base + e + 449:64], T.us_sb[:, e:32:4]))
-    t_uq = v([t_ut], lambda: V.quantize_mx(T.uq[:], T.up[:], T.ut[:]))
-    for i in (3, 2, 1, 0):
+    def zero_v(h, k=None):
+        c0, n = (1024 * h, 1024) if k is None else (1024 * h + 512 * k, 512)
+        t_z[h] = v([], lambda: V.memset(T.wm[:, c0:c0 + n], 0.0))
+
+    def quant_x(i):
         lo, hi = 128 * i, (608 if i == 3 else 128 * i + 128)
-        t_q = v([t_x[i]], lambda: V.quantize_mx(T.xq[:, lo:hi], T.xp[:, lo:hi], T.xb[:, 4 * lo:4 * hi]))
+        return v([t_x[i], t_f], lambda: V.quantize_mx(T.xq[:, lo:hi], T.xp[:, lo:hi], T.xb[:, 4 * lo:4 * hi]))
+    for k in range(2):
+        zero_a(ZA[0], k)
+    zero_v(ZV[0])
+    t_q = quant_x(3)
+
+    for e in range(4):
+        b0, b1 = 4 * 15 + e, 4 * (144 + 16) + e
+        t_ua = a([t_us, t_u0], lambda: S.activation(T.ut[:, b1:b1 + 449:64], T.us_sb[:, e:32:4], COPY))
+        t_ut = v([t_us, t_u0], lambda: V.tensor_copy(T.ut[:, b0:b0 + 449:64], T.us_sb[:, e:32:4]))
+    t_uq = v([t_ut, t_ua], lambda: V.quantize_mx(T.uq[:], T.up[:], T.ut[:]))
+    for i in (3, 2, 1, 0):
+        if i < 3:
+            t_q = quant_x(i)
         need("p", [t_uq, t_q])
         for k in (4 * i + 3, 4 * i + 2, 4 * i + 1, 4 * i):
             st = 15 - k if k % 2 else 144 + 16 - k
@@ -119,7 +122,8 @@ def rank_program(g, core, T, topo):
                 call()
             else:
                 t_sm = op("p", [], call, "px")
-    t_own = v([t_sm], lambda: V.tensor_copy(T.sc[:, 32 * r:32 * r + 32], T.ps0[:, 0:32]))
+    zero_v(ZV[1], 0)
+    t_own = v([t_sm], lambda: V.tensor_copy(T.sc[:, 32 * u:32 * u + 32], T.ps0[:, 0:32]))
 
     def send(dst, view, rsem, lsem):
         d = T.cores[dst]
@@ -135,105 +139,86 @@ def rank_program(g, core, T, topo):
         cnt[lsem] = cnt.get(lsem, 0) + len(topo.engines(core, ds[0]))
 
     need("g", [t_own])
-    send_all(T.sc[:, 32 * r:32 * r + 32], "s%d" % r, "sloc")
+    send_all(T.sc[:, 32 * u:32 * u + 32], "s%d" % r, "sloc")
     n_in = {s: len(topo.engines(T.cores[s], core)) for s in senders}
 
-    c1 = v([t_small], lambda: V.tensor_scalar(T.i15[:], T.ip[:], 15, None, A.bitwise_and))
-    c2 = v([], lambda: V.tensor_scalar(T.ial[:], T.ip[:], 15, 2, A.bitwise_and, A.arith_shift_right))
+    for h in ZA[1:]:
+        for k in range(2):
+            zero_a(h, k)
+    t_dc = a([t_dl], lambda: S.activation(T.dc[:], T.dl[:], IDENT, bias=0.5 - CAP * u))
+    zero_v(ZV[1], 1)
+    for h in ZV[2:]:
+        zero_v(h)
+    c2 = v([t_ip], lambda: V.tensor_scalar(T.ial[:], T.ip[:], 15, 2, A.bitwise_and, A.arith_shift_right))
     c3 = v([], lambda: V.tensor_scalar(T.it3[:], T.ip[:], 3, None, A.bitwise_and))
-    v([], lambda: V.tensor_scalar(T.m16[:], T.mi[:], 0.5, None, A.is_gt))
-    v([], lambda: V.tensor_scalar(T.m32[:], T.ni[:], 0.5, None, A.is_gt))
-    c4 = v([], lambda: V.tensor_scalar(T.k2[:], T.ki[:], 4.0, 4096.0, A.is_equal, A.mult))
-    c5 = v([c1], lambda: V.tensor_scalar(T.a32[:], T.i15[:], 32.0, None, A.mult))
+    v([], lambda: V.memset(T.ll[:, 0:240], 2048.0))
     c6 = v([c2], lambda: V.tensor_copy(T.alf[:], T.ial[:]))
     c7 = v([c3], lambda: V.tensor_copy(T.t3f[:], T.it3[:]))
-    v([c5], lambda: V.tensor_scalar(T.dl[:], T.bi[:], T.a32[:], None, A.add))
-    v([], lambda: V.tensor_scalar(T.dc[:], T.bi[:], T.a32[:], -1.3, A.add, A.add))
-    c8 = v([c6], lambda: V.tensor_scalar(T.k1[:], T.ki[:], T.alf[:], 4096.0, A.is_lt, A.mult))
-    t_const = v([c4, c8], lambda: V.tensor_tensor(T.kk[:], T.k1[:], T.k2[:], A.max))
-    t_vv = a([c7, t_vi], lambda: S.activation(T.vv[:], T.vi[:], IDENT, bias=T.t3f[:]))
+    v([], lambda: V.memset(T.rt[:, 0:32], 0.0))
+    t_f2 = v([], lambda: V.memset(T.rr[:, 159:1024:32], 0.0))
+    t_kk = v([c6, t_ki], lambda: V.tensor_scalar(T.kk[:], T.ki[:], T.alf[:], 4096.0, A.is_lt, A.mult))
+    t_w = {}
+    for h in WORD:
+        t_w[h // 2] = dma("s", [t_z[h]], T.wm[16 * h:16 * h + 16, 1024 * h:1024 * h + 1024], T.w[16 * h:16 * h + 16, :],
+                          "w%d" % (h // 2))
+    t_wq = {}
 
     def quant_w(i):
-        return v([t_w[i]], lambda: V.quantize_mx(T.wq[:, 512 * i:512 * i + 512], T.wp[:, 512 * i:512 * i + 512],
-                                                 T.wm[:, 2048 * i:2048 * i + 2048]))
-    for i in range(3):
-        t_wq = quant_w(i)
+        t_wq[i] = v([t_w[i]], lambda: V.quantize_mx(T.wq[:, 512 * i:512 * i + 512], T.wp[:, 512 * i:512 * i + 512],
+                                                    T.wm[:, 2048 * i:2048 * i + 2048]))
+    for i in QEARLY:
+        quant_w(i)
 
-    def score(s):
-        return T.sc[:, 32 * s:32 * s + 32]
-
-    def arrived(s):
-        return [("s%d" % s, n_in[s])]
-    conds = []
-    for side, buf, cbuf, cmp in ((lambda s: s < r, T.mx1, T.cl1, A.is_gt), (lambda s: s > r, T.mx2, T.cl2, A.is_ge)):
-        grp = [s for s in senders if side(s)]
-        if not grp:
-            continue
-        cur, tk = score(grp[0]), []
-        need("v", arrived(grp[0]))
-        for n, s in enumerate(grp[1:]):
-            nxt = buf[:] if n == 0 else T.win[:]
-            tk = [v(tk + arrived(s), lambda: V.tensor_tensor(nxt, cur, score(s), A.max))]
-            cur = nxt
-        conds.append((cbuf, v(tk + [t_own], lambda: V.tensor_tensor(cbuf[:], score(r), cur, cmp))))
-    if len(conds) == 2:
-        wn_ = T.win
-        t_win = v([conds[0][1], conds[1][1]], lambda: V.tensor_tensor(T.win[:], T.cl1[:], T.cl2[:], A.mult))
-    else:
-        wn_, t_win = conds[0]
-    m16a, m32a = T.m16[:, 0:32], T.m32[:, 0:32]
-    t1 = v([t_win, t_const], lambda: V.tensor_tensor_scan(T.ra[:], m32a, wn_[:], 0.0, A.mult, A.add))
-    b1 = v([], lambda: V.tensor_tensor(T.w2[:], wn_[:], T.dl[:], A.mult))
-    t2 = v([t1], lambda: V.transpose(T.rt[:, 32:64], T.ra[:]))
-    b2 = v([b1], lambda: V.tensor_tensor(T.u2[:], T.dc[:], T.w2[:], A.subtract))
-    t3 = v([t2], lambda: V.tensor_tensor_scan(T.ea[:], T.rt[:, 31:63], m16a, 0.0, A.add, A.mult))
-    b3 = v([b2], lambda: V.tensor_tensor(T.ta[:], T.u2[:], T.ra[:], A.add))
+    need("v", [("s%d" % s, n_in[s]) for s in senders])
+    m1 = v([t_own], lambda: V.tensor_tensor(T.m64[:], T.sc[:, 0:64], T.sc[:, 64:128], A.max))
+    m0 = v([], lambda: V.tensor_tensor(T.ab[:], T.sc[:, 64:128], T.sc[:, 0:64], A.is_gt))
+    v([m1], lambda: V.tensor_tensor(T.cc[:, 0:32], T.m64[:, 32:64], T.m64[:, 0:32], A.is_le))
+    m2 = v([], lambda: V.tensor_tensor(T.cc[:, 32:64], T.m64[:, 32:64], T.m64[:, 0:32], A.is_gt))
+    m3 = v([m2], lambda: V.tensor_tensor(T.ww[:, 64:128], T.ab[:], T.cc[:], A.mult))
+    t_ww = v([m3], lambda: V.tensor_tensor(T.ww[:, 0:64], T.cc[:], T.ww[:, 64:128], A.subtract))
+    win = T.ww[:, 32 * u:32 * u + 32]
+    t1 = v([t_ww, t_gc], lambda: V.tensor_tensor_scan(T.rr[:, 0:128], T.m32[:], T.ww[:], 0.0, A.mult, A.add))
+    b1 = v([], lambda: V.tensor_tensor(T.w2[:], win, T.dl[:], A.mult))
+    t2 = v([t1, t_f2], lambda: V.transpose(T.rt[:, 32:64], T.rr[:, 31:1024:32]))
+    b2 = v([b1, t_dc], lambda: V.tensor_tensor(T.u2[:], T.dc[:], T.w2[:], A.subtract))
+    t3 = v([t2], lambda: V.tensor_tensor_scan(T.ea[:], T.rt[:, 31:63], T.lim[:], 1e6, A.add, A.min))
+    b3 = v([b2], lambda: V.tensor_tensor(T.ta[:], T.u2[:], T.rr[:, 32 * u:32 * u + 32], A.add))
     t4 = v([t3], lambda: V.transpose(T.et[:], T.ea[:]))
-    m1 = v([], lambda: V.tensor_tensor(T.m64[:], T.sc[:, 0:64], T.sc[:, 64:128], A.max))
-    t5 = v([t4, b3], lambda: V.tensor_scalar(T.oi[:], T.ta[:], T.et[:, 31:32], 1.25, A.add, A.mult))
-    m2 = v([m1], lambda: V.tensor_tensor(T.mm[:], T.m64[:, 0:32], T.m64[:, 32:64], A.max))
-    t6 = v([t5], lambda: V.tensor_copy(T.ou[:], T.oi[:]))
-    n2 = v([m2], lambda: V.tensor_tensor(T.ne[:, 64:96], score(2), T.mm[:], A.not_equal))
-    t7 = v([t6, t_vv], lambda: V.tensor_copy(T.ll[:].indirect(T.ou[:]), T.vv[:]))
-    n1 = v([], lambda: V.tensor_tensor(T.ne[:, 32:64], score(1), T.mm[:], A.not_equal))
-    t8 = v([t7], lambda: V.tensor_tensor_scan(T.sl5[:], T.ll[:, 0:240], T.kk[:], 4096.0, A.min, A.max))
-    n0 = v([], lambda: V.tensor_tensor(T.ne[:, 0:32], score(0), T.mm[:], A.not_equal))
-    t9 = v([t8], lambda: V.tensor_copy(T.offa[:], T.sl5[:, 3:240:5]))
-    q2 = v([n2], lambda: V.tensor_scalar(T.q2[:], T.ne[:, 64:96], 1.0, None, A.add))
+    t6 = v([t4, b3], lambda: V.tensor_scalar(T.ou[:], T.ta[:], T.et[:, u:u + 1], 1.25, A.add, A.mult))
+    t7 = v([t6], lambda: V.tensor_copy(T.ll[:].indirect(T.ou[:]), T.vi[:]))
+    t8 = v([t7, t_kk], lambda: V.tensor_tensor_scan(T.sl5[:], T.ll[:, 0:240], T.kk[:], 4096.0, A.min, A.max))
+    t9 = v([t8, c7], lambda: V.tensor_scalar(T.offa[:], T.sl5[:, 4:240:5], T.t3f[:], None, A.add))
     t10 = a([t9], lambda: S.activation(T.cb[:, 384:768], T.xb[:].indirect(T.offa[:, 24:48]), COPY))
     t11 = v([t9], lambda: V.tensor_copy(T.cb[:, 0:384], T.xb[:].indirect(T.offa[:, 0:24])))
-    q1 = v([q2, n1], lambda: V.tensor_tensor(T.q1[:], T.ne[:, 32:64], T.q2[:], A.mult))
-    lo = CAP * r
+    lo = CAP * u
     t_c = v([t10, t11], lambda: V.quantize_mx(T.lq[:, lo:lo + CAP], T.lp[:, lo:lo + CAP], T.cb[:]))
     need("g", [t_c])
     for d in peers:
         send(d, T.lq[:, lo:lo + CAP].bitcast(dt.uint8), "c%d" % r, "cloc")
         send(d, T.lp[:, lo:lo + CAP], "c%d" % r, "cloc")
-    t_wq3 = quant_w(3)
+    for i in range(4):
+        if i not in QEARLY:
+            quant_w(i)
 
-    t = v([q1], lambda: V.tensor_scalar(T.q0[:], T.q1[:], 1.0, None, A.add))
-    t_wn = v([t, n0], lambda: V.tensor_tensor(T.wnt[:], T.ne[:, 0:32], T.q0[:], A.mult))
-    for s in range(NR):
-        t = v([t_wn], lambda: V.tensor_scalar(T.ww[:, 32 * s:32 * s + 32], T.wnt[:], float(s), None, A.is_equal))
-    t = v([t], lambda: V.tensor_tensor_scan(T.rr[:], T.m32[:], T.ww[:], 0.0, A.mult, A.add))
-    t = v([t], lambda: V.transpose(T.rt4[:, 32:160], T.rr[:]))
-    t = v([t], lambda: V.tensor_tensor_scan(T.e4[:], T.rt4[:, 31:159], T.m16[:], 0.0, A.add, A.mult))
-    t = v([t], lambda: V.transpose(T.et4[:], T.e4[:]))
     for s in range(NR):
         c = 32 * s
-        tp = v([t], lambda: V.tensor_scalar(T.p4[:, c:c + 32], T.rr[:, c:c + 32], T.et4[:, c + 31:c + 32],
-                                            float(CAP * s - 1), A.add, A.add))
+        tp = v([], lambda: V.tensor_scalar(T.p4[:, c:c + 32], T.rr[:, c:c + 32], T.et[:, s:s + 1], None, A.add))
+    q1 = v([], lambda: V.tensor_tensor(T.q1[:], T.ww[:, 64:96], T.ww[:, 96:128], A.add))
     t = v([tp], lambda: V.tensor_tensor(T.pm[:], T.p4[:], T.ww[:], A.mult))
+    q2 = v([q1], lambda: V.tensor_tensor(T.q2[:], T.q1[:], T.cc[:, 32:64], A.add))
     t = v([t], lambda: V.tensor_tensor(T.ph[:], T.pm[:, 0:64], T.pm[:, 64:128], A.add))
-    t = v([t], lambda: V.tensor_tensor(T.pi[:], T.ph[:, 0:32], T.ph[:, 32:64], A.add))
-    t_pt = v([t], lambda: V.transpose(T.ptr[:], T.pi[:]))
-    for ab in range(4):
-        for bh in range(2):
-            p0, c0 = 32 * ab + 16 * bh, 128 * bh + 32 * ab
-            t_d2 = dma("s", [t_pt], T.d2[0:16, c0:c0 + 32], T.ptr[p0:p0 + 16, :], "d2s")
-    for k in range(8):
-        t_zz = dma("s", [t_d2], T.zz[16 * k:16 * k + 16, :], T.d2[:], "zs")
-    dma("s", [t_wn], T.wn[:], T.wnt[:], "wn")
+    t_wn = v([q2], lambda: V.tensor_tensor(T.wnt[:], T.q2[:], T.cc[:, 32:64], A.add))
+    for k in range(4):
+        c = 16 * (k // 2)
+        td = v([t], lambda: V.tensor_tensor(T.dd[:, 16 * k:16 * k + 16], T.ph[:, c:c + 16], T.ph[:, 32 + c:48 + c], A.add))
+    t = v([td], lambda: V.transpose(T.xf[:], T.dd[:]))
+    for k in range(2):
+        t_xu = v([t], lambda: V.tensor_copy(T.xu[:, k:64:2], T.xf[:, 32 * k:32 * k + 32]))
+    t_ob = {}
+    for b in (3, 0, 1, 2):
+        for d in range(4):
+            t_ob[b] = dma("s", [t_xu], T.offb[32 * d:32 * d + 32, 64 * b:64 * b + 64], T.xu[32 * b:32 * b + 32, :], "ob%d" % b)
+    dma("g", [t_wn], T.wn[:], T.wnt[:], "wn")
 
     banks = {"v": [T.ps0, T.ps1, T.ps2, T.ps3], "a": [T.ps4, T.ps5, T.ps6, T.ps7]}
     hist = {"v": [], "a": []}
@@ -243,8 +228,8 @@ def rank_program(g, core, T, topo):
         n = len(hist[e])
         bank = banks[e][n % 4]
         old = [hist[e][n - 4]] if n >= 4 else [t_own]
-        w0, c0 = 256 * h + 128 * o, CAP * s
-        tk = op("p", deps + old + [t_wq if h < 6 else t_wq3], lambda: g.tensor.matmul_mx(
+        w0, c0 = 256 * h + 128 * o, CAP * SLOT[s]
+        tk = op("p", deps + old + [t_wq[h // 2]], lambda: g.tensor.matmul_mx(
             bank[:, 0:CAP], T.wq[:, w0:w0 + 128], T.wp[:, w0:w0 + 128], T.lq[:, c0:c0 + CAP], T.lp[:, c0:c0 + CAP],
             True, True), "p" + e)
         d0 = RW * (2 * h + o) + c0
@@ -260,43 +245,39 @@ def rank_program(g, core, T, topo):
         return T.rw[:, d0:d0 + RW]
 
     def rdeps(h, o):
-        return [ready[(s, h, o)] for s in range(NR)]
+        return [ready[(s, h, o)] for s in range(NR)] + [t_ob[h // 2]]
 
     jobs = [(h, o) for h in range(8) for o in range(2)]
-    for n, (h, o) in enumerate(jobs):
-        product(r, h, o, "v" if n % 4 == 3 else "a", [t_c])
-    for s in senders[:2]:
-        for n, (h, o) in enumerate(jobs):
-            product(s, h, o, "v" if n % 2 else "a", [("c%d" % s, 2 * n_in[s])])
-    for bh in range(2):
-        t_ob = v([t_zz], lambda: V.tensor_copy(T.offb[:, bh:256:2], T.zz[:, 128 * bh:128 * bh + 128]))
+    for s, who in zip([r] + senders[:2], COPIES):
+        for (h, o), e in zip(jobs, who):
+            product(s, h, o, e, [t_c] if s == r else [("c%d" % s, 2 * n_in[s])])
     s = senders[2]
     dep = [("c%d" % s, 2 * n_in[s])]
 
     def gath(out, h, o):
-        return a(rdeps(h, o) + [t_ob], lambda: S.activation(out[:], window(h, o).indirect(T.offb[:, 32 * h:32 * h + 32]), COPY))
-    for h, o, e in ((7, 0, "a"), (0, 0, "v"), (1, 0, "v")):
-        product(s, h, o, e, dep)
-    t_g0 = gath(T.g0, 7, 0)
-    for h, o, e in ((5, 0, "a"), (2, 0, "v"), (3, 0, "v"), (6, 0, "a"), (4, 0, "v"), (0, 1, "v"), (1, 1, "v")):
-        product(s, h, o, e, dep)
-    t_g5 = gath(T.g5, 5, 0)
-    t_g6 = gath(T.g6, 6, 0)
-    t_ga = op("g", [t_g5, t_g6], lambda: g.dma_start(T.g6[:], T.g5[:], accum_op=A.add), "ga", 16)
-    product(s, 7, 1, "a", dep)
-    t_g1 = gath(T.g1, 7, 1)
-    for h in (2, 3, 4, 5, 6):
-        product(s, h, 1, "a", dep)
+        return a(rdeps(h, o), lambda: S.activation(out[:], window(h, o).indirect(T.offb[:, 32 * h:32 * h + 32]), COPY))
+    got = {}
+    for step in LAST:
+        h, o = int(step[1]), int(step[2])
+        if step[0] == "g":
+            got[(h, o)] = gath(T[GBUF[(h, o)]], h, o)
+        else:
+            product(s, h, o, step[0], dep)
 
-    cur, tk = T.g0, [t_g0]
-    for h in range(5):
-        out = (T.ac0, T.ac1)[h % 2]
-        tk = [v(tk + rdeps(h, 0) + [t_ob], lambda: V.tensor_tensor(
+    def add_dma(deps, out, in_, sem):
+        return op("g", deps, lambda: g.dma_start(out, in_, accum_op=A.add), sem, 16)
+    t_ga = add_dma([got[(5, 0)], got[(6, 0)]], T.g6[:], T.g5[:], "ga")
+    cur, tk = T.g0, [got[(7, 0)]]
+    for n, h in enumerate(h for h in range(7) if (h, 0) not in got):
+        out = (T.ac0, T.ac1)[n % 2]
+        tk = [v(tk + rdeps(h, 0), lambda: V.tensor_tensor(
             out[:], window(h, 0).indirect(T.offb[:, 32 * h:32 * h + 32]), cur[:], A.add))]
         cur = out
     t_y0 = dma("s", tk, T.y[:, 0:512], cur[:], "y0")
-    op("g", [t_ga, t_y0], lambda: g.dma_start(T.y[:, 0:512], T.g6[:], accum_op=A.add), "ga", 16)
-    cur, tk = T.g1, [t_g1]
+    if (4, 0) in got:
+        t_y0 = add_dma([t_y0, got[(4, 0)]], T.y[:, 0:512], T.g4[:], "gb")
+    add_dma([t_ga, t_y0], T.y[:, 0:512], T.g6[:], "gc_")
+    cur, tk = T.g1, [got[(7, 1)]]
     for h in range(6):
         out = (T.ac2, T.ac3)[h % 2]
         tk = [v(tk + rdeps(h, 1), lambda: V.tensor_tensor(
@@ -309,3 +290,13 @@ def rank_program(g, core, T, topo):
         dma(("s", "a")[k], [t_l], T.y[:, 512 + c0:768 + c0], T.ac2[:, c0:c0 + 256], "y%d" % (1 + k))
 
     need("g", sorted(cnt.items()))
+
+
+ZA = (0, 1, 4, 6)
+ZV = (2, 3, 5, 7)
+WORD = (0, 2, 1, 4, 3, 5, 6, 7)
+QEARLY = (0, 1, 2)
+COPIES = ("aaaaaaavavavavav", "vavavavavavavava", "vavavavavavavava")
+GBUF = {(7, 0): "g0", (7, 1): "g1", (6, 0): "g6", (5, 0): "g5", (4, 0): "g4"}
+LAST = ("a70", "v00", "v10", "v20", "v30", "g70", "a60", "a50", "a40", "g60", "g50", "a71", "g71", "a01", "a11", "a21", "a31", "a41",
+        "a51", "a61")

@@ -14,7 +14,7 @@ _sb = {
     "cb": (4 * CAP, BF), "lq": (RW, X4), "lp": (RW, U8), "sc": (128, F),
     "ip": (1, I32), "ial": (1, I32), "it3": (1, I32), "alf": (1, F), "t3f": (1, F),
     "vi": (512, F), "dl": (32, F), "dc": (32, F), "ki": (240, F), "kk": (240, F), "one": (128, F), "m32": (128, F), "lim": (32, F),
-    "ab": (64, F), "m64": (64, F), "cc": (64, F), "ww": (128, F), "rr": (1024, F), "rt": (64, F), "ea": (32, F), "et": (32, F),
+    "ab": (128, F), "m64": (64, F), "cc": (64, F), "ww": (128, F), "rr": (1024, F), "rt": (64, F), "ea": (32, F), "et": (32, F),
     "w2": (32, F), "u2": (32, F), "ta": (32, F), "oi": (32, I32), "ou": (32, U16), "ll": (LW, F), "sl5": (240, F), "offa": (48, U16),
     "p4": (128, F), "pm": (128, F), "ph": (64, F), "dd": (64, F), "xf": (64, F), "xu": (64, U16), "offb": (256, U16),
     "q1": (32, F), "q2": (32, F), "wnt": (32, F),
@@ -24,7 +24,7 @@ _sb = {
 SCRATCH = {k: ("sbuf", [128, n], d) for k, (n, d) in _sb.items()}
 for _k in range(8):
     SCRATCH["ps%d" % _k] = ("psum", [128, 512], F)
-SEMAPHORES = (["v", "a", "pv", "pa", "px", "gi", "us", "wn", "ob0", "ob1", "ob2", "ob3", "ga", "gb", "gc_", "y0", "y1", "y2", "sloc", "cloc"]
+SEMAPHORES = (["v", "a", "pv", "pa", "px", "gi", "us", "wn", "ob0", "ob1", "ob2", "ob3", "ga", "gb", "gc_", "y0", "y1", "y2", "sloc", "cl0", "cl1", "cl2"]
               + ["x%d" % i for i in range(4)] + ["w%d" % i for i in range(4)]
               + ["s%d" % i for i in range(4)] + ["c%d" % i for i in range(4)])
 
@@ -171,11 +171,12 @@ def rank_program(g, core, T, topo):
 
     need("v", [("s%d" % s, n_in[s]) for s in senders])
     m1 = v([t_own], lambda: V.tensor_tensor(T.m64[:], T.sc[:, 0:64], T.sc[:, 64:128], A.max))
-    m0 = v([], lambda: V.tensor_tensor(T.ab[:], T.sc[:, 64:128], T.sc[:, 0:64], A.is_gt))
+    v([], lambda: V.tensor_tensor(T.ab[:, 64:128], T.sc[:, 64:128], T.sc[:, 0:64], A.is_gt))
     v([m1], lambda: V.tensor_tensor(T.cc[:, 0:32], T.m64[:, 32:64], T.m64[:, 0:32], A.is_le))
     m2 = v([], lambda: V.tensor_tensor(T.cc[:, 32:64], T.m64[:, 32:64], T.m64[:, 0:32], A.is_gt))
-    m3 = v([m2], lambda: V.tensor_tensor(T.ww[:, 64:128], T.ab[:], T.cc[:], A.mult))
-    t_ww = v([m3], lambda: V.tensor_tensor(T.ww[:, 0:64], T.cc[:], T.ww[:, 64:128], A.subtract))
+    m0 = v([], lambda: V.tensor_tensor(T.ab[:, 0:64], T.sc[:, 64:128], T.sc[:, 0:64], A.is_le))
+    v([m2], lambda: V.tensor_tensor(T.ww[:, 64:128], T.ab[:, 64:128], T.cc[:], A.mult))
+    t_ww = v([m0], lambda: V.tensor_tensor(T.ww[:, 0:64], T.ab[:, 0:64], T.cc[:], A.mult))
     win = T.ww[:, 32 * u:32 * u + 32]
     t1 = v([t_ww, t_gc], lambda: V.tensor_tensor_scan(T.rr[:, 0:128], T.m32[:], T.ww[:], 0.0, A.mult, A.add))
     b1 = v([], lambda: V.tensor_tensor(T.w2[:], win, T.dl[:], A.mult))
@@ -184,40 +185,41 @@ def rank_program(g, core, T, topo):
     t3 = v([t2], lambda: V.tensor_tensor_scan(T.ea[:], T.rt[:, 31:63], T.lim[:], 1e6, A.add, A.min))
     b3 = v([b2], lambda: V.tensor_tensor(T.ta[:], T.u2[:], T.rr[:, 32 * u:32 * u + 32], A.add))
     t4 = v([t3], lambda: V.transpose(T.et[:], T.ea[:]))
+    for s in range(NR):
+        c = 32 * s
+        tp = a([t4], lambda: S.activation(T.p4[:, c:c + 32], T.rr[:, c:c + 32], IDENT, bias=T.et[:, s:s + 1]))
+    q1 = v([], lambda: V.tensor_tensor(T.q1[:], T.ww[:, 64:96], T.ww[:, 96:128], A.add))
     t6 = v([t4, b3], lambda: V.tensor_scalar(T.ou[:], T.ta[:], T.et[:, u:u + 1], 1.25, A.add, A.mult))
+    q2 = v([q1], lambda: V.tensor_tensor(T.q2[:], T.q1[:], T.cc[:, 32:64], A.add))
     t7 = v([t6], lambda: V.tensor_copy(T.ll[:].indirect(T.ou[:]), T.vi[:]))
+    t_wn = v([q2], lambda: V.tensor_tensor(T.wnt[:], T.q2[:], T.cc[:, 32:64], A.add))
     t8 = v([t7, t_kk], lambda: V.tensor_tensor_scan(T.sl5[:], T.ll[:, 0:240], T.kk[:], 4096.0, A.min, A.max))
+    v([tp], lambda: V.tensor_tensor(T.pm[:, 0:64], T.p4[:, 0:64], T.ww[:, 0:64], A.mult))
     t9 = v([t8, c7], lambda: V.tensor_scalar(T.offa[:], T.sl5[:, 4:240:5], T.t3f[:], None, A.add))
     t10 = a([t9], lambda: S.activation(T.cb[:, 384:768], T.xb[:].indirect(T.offa[:, 24:48]), COPY))
+    t = v([], lambda: V.tensor_tensor(T.pm[:, 64:128], T.p4[:, 64:128], T.ww[:, 64:128], A.mult))
     t11 = v([t9], lambda: V.tensor_copy(T.cb[:, 0:384], T.xb[:].indirect(T.offa[:, 0:24])))
+    t = v([t], lambda: V.tensor_tensor(T.ph[:], T.pm[:, 0:64], T.pm[:, 64:128], A.add))
     lo = CAP * u
     t_c = v([t10, t11], lambda: V.quantize_mx(T.lq[:, lo:lo + CAP], T.lp[:, lo:lo + CAP], T.cb[:]))
     need("g", [t_c])
-    for d in peers:
-        send(d, T.lq[:, lo:lo + CAP].bitcast(dt.uint8), "c%d" % r, "cloc")
-        send(d, T.lp[:, lo:lo + CAP], "c%d" % r, "cloc")
-    for i in range(4):
-        if i not in QEARLY:
-            quant_w(i)
+    for n, d in enumerate(peers):
+        send(d, T.lq[:, lo:lo + CAP].bitcast(dt.uint8), "c%d" % r, "cl%d" % n)
+        send(d, T.lp[:, lo:lo + CAP], "c%d" % r, "cl%d" % n)
 
-    for s in range(NR):
-        c = 32 * s
-        tp = v([], lambda: V.tensor_scalar(T.p4[:, c:c + 32], T.rr[:, c:c + 32], T.et[:, s:s + 1], None, A.add))
-    q1 = v([], lambda: V.tensor_tensor(T.q1[:], T.ww[:, 64:96], T.ww[:, 96:128], A.add))
-    t = v([tp], lambda: V.tensor_tensor(T.pm[:], T.p4[:], T.ww[:], A.mult))
-    q2 = v([q1], lambda: V.tensor_tensor(T.q2[:], T.q1[:], T.cc[:, 32:64], A.add))
-    t = v([t], lambda: V.tensor_tensor(T.ph[:], T.pm[:, 0:64], T.pm[:, 64:128], A.add))
-    t_wn = v([q2], lambda: V.tensor_tensor(T.wnt[:], T.q2[:], T.cc[:, 32:64], A.add))
     for k in range(4):
         c = 16 * (k // 2)
         td = v([t], lambda: V.tensor_tensor(T.dd[:, 16 * k:16 * k + 16], T.ph[:, c:c + 16], T.ph[:, 32 + c:48 + c], A.add))
+    for i in range(4):
+        if i not in QEARLY:
+            quant_w(i)
     t = v([td], lambda: V.transpose(T.xf[:], T.dd[:]))
     for k in range(2):
         t_xu = v([t], lambda: V.tensor_copy(T.xu[:, k:64:2], T.xf[:, 32 * k:32 * k + 32]))
     t_ob = {}
     for b in (3, 0, 1, 2):
         for d in range(4):
-            t_ob[b] = dma("s", [t_xu], T.offb[32 * d:32 * d + 32, 64 * b:64 * b + 64], T.xu[32 * b:32 * b + 32, :], "ob%d" % b)
+            t_ob[b] = dma("s", [t_xu, ("cl0", cnt["cl0"])], T.offb[32 * d:32 * d + 32, 64 * b:64 * b + 64], T.xu[32 * b:32 * b + 32, :], "ob%d" % b)
     dma("g", [t_wn], T.wn[:], T.wnt[:], "wn")
 
     banks = {"v": [T.ps0, T.ps1, T.ps2, T.ps3], "a": [T.ps4, T.ps5, T.ps6, T.ps7]}
@@ -254,40 +256,48 @@ def rank_program(g, core, T, topo):
     s = senders[2]
     dep = [("c%d" % s, 2 * n_in[s])]
 
-    def gath(out, h, o):
-        return a(rdeps(h, o), lambda: S.activation(out[:], window(h, o).indirect(T.offb[:, 32 * h:32 * h + 32]), COPY))
-    got = {}
-    for step in LAST:
-        h, o = int(step[1]), int(step[2])
-        if step[0] == "g":
-            got[(h, o)] = gath(T[GBUF[(h, o)]], h, o)
-        else:
-            product(s, h, o, step[0], dep)
-
     def add_dma(deps, out, in_, sem):
         return op("g", deps, lambda: g.dma_start(out, in_, accum_op=A.add), sem, 16)
-    t_ga = add_dma([got[(5, 0)], got[(6, 0)]], T.g6[:], T.g5[:], "ga")
-    cur, tk = T.g0, [got[(7, 0)]]
-    for n, h in enumerate(h for h in range(7) if (h, 0) not in got):
-        out = (T.ac0, T.ac1)[n % 2]
-        tk = [v(tk + rdeps(h, 0), lambda: V.tensor_tensor(
-            out[:], window(h, 0).indirect(T.offb[:, 32 * h:32 * h + 32]), cur[:], A.add))]
-        cur = out
-    t_y0 = dma("s", tk, T.y[:, 0:512], cur[:], "y0")
-    if (4, 0) in got:
-        t_y0 = add_dma([t_y0, got[(4, 0)]], T.y[:, 0:512], T.g4[:], "gb")
-    add_dma([t_ga, t_y0], T.y[:, 0:512], T.g6[:], "gc_")
-    cur, tk = T.g1, [got[(7, 1)]]
-    for h in range(6):
-        out = (T.ac2, T.ac3)[h % 2]
-        tk = [v(tk + rdeps(h, 1), lambda: V.tensor_tensor(
-            out[:], window(h, 1).indirect(T.offb[:, 32 * h:32 * h + 32]), cur[:], A.add))]
-        cur = out
-    for k in range(2):
-        c0 = 256 * k
-        t_l = v(tk + rdeps(6, 1), lambda: V.tensor_tensor(
-            T.ac2[:, c0:c0 + 256], window(6, 1).indirect(T.offb[:, 192 + 16 * k:192 + 16 * k + 16]), cur[:, c0:c0 + 256], A.add))
-        dma(("s", "a")[k], [t_l], T.y[:, 512 + c0:768 + c0], T.ac2[:, c0:c0 + 256], "y%d" % (1 + k))
+
+    got = {}
+    cur = {}
+    left = [sum(1 for st in TAIL if st[0] == "s" and int(st[2]) == o and st[3:] != "h") for o in range(2)]
+    done = [0, 0]
+    for step in TAIL:
+        h, o = int(step[1]), int(step[2])
+        halves = {"": (0, 1), "l": (0,), "h": (1,)}[step[3:]]
+        c0, c1 = 256 * halves[0], 256 * halves[-1] + 256
+        picked = window(h, o).indirect(T.offb[:, 32 * h + c0 // 16:32 * h + c1 // 16])
+        if step[0] == "g":
+            out = T[GBUF[(h, o)]]
+            got[(h, o)] = a(rdeps(h, o), lambda: S.activation(out[:, c0:c1], picked, COPY))
+            if h == 7:
+                for k in halves:
+                    cur[(o, k)] = (out, got[(h, o)])
+            if (5, 0) in got and (6, 0) in got and "g" not in cur:
+                cur["g"] = add_dma([got[(5, 0)], got[(6, 0)]], T.g6[:], T.g5[:], "ga")
+                if Y0 == "g":
+                    t_y0 = dma("s", [cur["g"]], T.y[:, 0:512], T.g6[:], "y0")
+        elif step[0] == "s":
+            if step[3:] != "h":
+                done[o] += 1
+            out = T["ac%d" % (2 * o + done[o] % 2)]
+            src = cur[(o, halves[0])][0]
+            tk = v([cur[(o, k)][1] for k in halves] + rdeps(h, o), lambda: V.tensor_tensor(out[:, c0:c1], picked, src[:, c0:c1], A.add))
+            for k in halves:
+                cur[(o, k)] = (out, tk)
+            if done[o] == left[o]:
+                if o == 1:
+                    dma(("s", "a")[halves[0]], [tk], T.y[:, 512 + c0:512 + c1], out[:, c0:c1], "y%d" % (1 + halves[0]))
+                elif halves == (0,):
+                    pass
+                elif Y0 == "g":
+                    add_dma([tk, t_y0], T.y[:, 0:512], out[:], "gb")
+                else:
+                    t_y0 = dma("s", [tk], T.y[:, 0:512], out[:], "y0")
+                    add_dma([cur["g"], t_y0], T.y[:, 0:512], T.g6[:], "gb")
+        else:
+            product(s, h, o, step[0], dep)
 
     need("g", sorted(cnt.items()))
 
@@ -296,7 +306,8 @@ ZA = (0, 1, 4, 6)
 ZV = (2, 3, 5, 7)
 WORD = (0, 2, 1, 4, 3, 5, 6, 7)
 QEARLY = (0, 1, 2)
-COPIES = ("aaaaaaavavavavav", "vavavavavavavava", "vavavavavavavava")
-GBUF = {(7, 0): "g0", (7, 1): "g1", (6, 0): "g6", (5, 0): "g5", (4, 0): "g4"}
-LAST = ("a70", "v00", "v10", "v20", "v30", "g70", "a60", "a50", "a40", "g60", "g50", "a71", "g71", "a01", "a11", "a21", "a31", "a41",
-        "a51", "a61")
+COPIES = ("aavavavavavavava", "vavavavavavavava", "vavavavavavavava")
+GBUF = {(7, 0): "g0", (7, 1): "g1", (6, 0): "g6", (5, 0): "g5"}
+Y0 = "v"
+TAIL = ("a70 v00 a60 v10 v20 g70l g70h a50 g60 a30 a40 g50 a71 a01 g71 a11 a21 a31 a41 a51 a61".split()
+        + ["s%d%d%s" % (h, o, k) for o, n in ((0, 5), (1, 7)) for h in range(n) for k in "lh"])

@@ -13,20 +13,35 @@ _sb = {
     "zt": (512, BF), "wm": (8192, BF), "wq": (2048, X4), "wp": (2048, U8),
     "cb": (4 * CAP, BF), "lq": (RW, X4), "lp": (RW, U8), "sc": (128, F),
     "ip": (1, I32), "ial": (1, I32), "it3": (1, I32), "alf": (1, F), "t3f": (1, F),
-    "vi": (512, F), "dl": (32, F), "dc": (32, F), "ki": (240, F), "kk": (240, F), "one": (128, F), "m32": (128, F), "lim": (32, F),
-    "ab": (128, F), "m64": (64, F), "cc": (64, F), "ww": (128, F), "rr": (1024, F), "rt": (64, F), "ea": (32, F), "et": (32, F),
-    "w2": (32, F), "u2": (32, F), "ta": (32, F), "oi": (32, I32), "ou": (32, U16), "ll": (LW, F), "sl5": (240, F), "offa": (48, U16),
+    "vi": (512, F), "dl": (32, F), "dc": (32, F), "ki": (240, F), "kk": (240, F), "m32": (128, F), "lim": (32, F),
+    "c1": (32, F), "c2": (32, F), "c3": (32, F), "c12": (32, F), "win": (32, F), "ra": (32, F), "rt": (64, F), "ea": (32, F),
+    "et": (32, F), "w2": (32, F), "u2": (32, F), "ta": (32, F), "ou": (32, U16), "ll": (LW, F), "sl5": (240, F), "offa": (48, U16),
+    "ab": (128, F), "m64": (64, F), "cc": (64, F), "ww": (128, F), "rr": (1024, F), "rt4": (64, F), "e4": (32, F), "et4": (32, F),
     "p4": (128, F), "pm": (128, F), "ph": (64, F), "dd": (64, F), "xf": (64, F), "xu": (64, U16), "offb": (256, U16),
     "q1": (32, F), "q2": (32, F), "wnt": (32, F),
-    "rw": (16 * RW, F), "g0": (512, F), "g1": (512, F), "g4": (512, F), "g5": (512, F), "g6": (512, F), "ac0": (512, F),
+    "rw": (16 * RW, F), "g0": (512, F), "g1": (512, F), "g5": (512, F), "g6": (512, F), "ac0": (512, F),
     "ac1": (512, F), "ac2": (512, F), "ac3": (512, F),
 }
 SCRATCH = {k: ("sbuf", [128, n], d) for k, (n, d) in _sb.items()}
 for _k in range(8):
     SCRATCH["ps%d" % _k] = ("psum", [128, 512], F)
-SEMAPHORES = (["v", "a", "pv", "pa", "px", "gi", "us", "wn", "ob0", "ob1", "ob2", "ob3", "ga", "gb", "gc_", "y0", "y1", "y2", "sloc", "cl0", "cl1", "cl2"]
-              + ["x%d" % i for i in range(4)] + ["w%d" % i for i in range(4)]
-              + ["s%d" % i for i in range(4)] + ["c%d" % i for i in range(4)])
+SEMAPHORES = (["v", "a", "pv", "pa", "px", "gi", "us", "wn", "ga", "gb", "y0", "y1", "y2", "sloc"]
+              + [n + str(i) for n in ("x", "w", "s", "c", "ob", "cl") for i in range(4)])
+
+ZA = (0, 1, 4, 6, 7)
+ZV = (2, 3, 5)
+WORD = (0, 2, 1, 3, 4, 5, 6, 7)
+QEARLY = (0, 1, 2)
+GBUF = {(7, 0): "g0", (7, 1): "g1", (6, 0): "g6", (5, 0): "g5"}
+_JOBS = ["%d%d" % (h, o) for h in range(8) for o in range(2)]
+_NEED = "70 00 10 60 20 50 30 40 71 01 11 21 31 41 51 61".split()
+PLAN = ("L L Q a000 a001 L a010 v011 L L L L a020 v021 L a030 v031 L L".split()
+        + [e + "0" + j for e, j in zip("va" * 4, _JOBS[8:])]
+        + [e + "1" + j for e, j in zip("va" * 8, _NEED)]
+        + [e + "2" + j for e, j in zip("va" * 8, _NEED[:9])]
+        + "a370 v300 a360 v310 g70l v320 g70h v330 a350 g60 a371 g50 a340 g71".split()
+        + ["a" + k + j for j in _NEED[9:] for k in "23"]
+        + ["s%d%d%s" % (h, o, k) for o, n in ((0, 5), (1, 7)) for h in range(n) for k in "lh"])
 
 
 def rank_program(g, core, T, topo):
@@ -64,6 +79,9 @@ def rank_program(g, core, T, topo):
     def dma(qn, deps, out, in_, sem):
         return op(qn, deps, lambda: Q[qn].dma_start(out, in_), sem, 16)
 
+    def tt(deps, out, in0, in1, alu):
+        return v(deps, lambda: V.tensor_tensor(out, in0, in1, alu))
+
     peers = [(r + k) % NR for k in (1, 2, 3)]
     senders = [(r - k) % NR for k in (1, 2, 3)]
     u = SLOT[r]
@@ -74,15 +92,13 @@ def rank_program(g, core, T, topo):
         t_x[i] = dma(qn, [], T.xb[:, 512 * i:512 * i + 512], T.x[:, 512 * i:512 * i + 512], "x%d" % i)
 
     def io(out, pattern, base, cm):
-        return op("g", [("gi", cnt.get("gi", 0))], lambda: g.iota(out, pattern, base, cm, allow_small_or_imprecise_dtypes=True), "gi")
+        return op("g", [], lambda: g.iota(out, pattern, base, cm, allow_small_or_imprecise_dtypes=True), "gi")
     t_ip = io(T.ip[:], [[0, 1]], 0, 1)
     t_ki = io(T.ki[:], [[0, 48], [1, 5]], -1, 0)
     t_dl = io(T.dl[:], [[1, 32]], 200, 32)
-    t_one = io(T.one[:], [[0, 128]], 1, 0)
-    for b in range(4):
-        io(T.lim[32 * b:32 * b + 32, :], [[0, 2], [4096, 16]], -1, CAP)
-    op("g", [("gi", cnt["gi"])], lambda: g.affine_select(T.m32[:], T.one[:], [[0, 4], [1, 32]], A.is_gt, 0.0, 0, 0), "gi")
-    t_gc = io(T.vi[:], [[4, 32], [128, 16]], 0, 0)
+    io(T.lim[:], [[0, 2], [4096, 16]], 0, 0)
+    t_gc = io(T.m32[:], [[0, 4], [4096, 32]], 0, 0)
+    t_vi = io(T.vi[:], [[4, 32], [128, 16]], 0, 0)
 
     t_zt = v([], lambda: V.memset(T.zt[:], 0.0))
     t_u0 = v([], lambda: V.memset(T.ut[:], 0.0))
@@ -103,12 +119,12 @@ def rank_program(g, core, T, topo):
     for k in range(2):
         zero_a(ZA[0], k)
     zero_v(ZV[0])
-    t_q = quant_x(3)
 
     for e in range(4):
         b0, b1 = 4 * 15 + e, 4 * (144 + 16) + e
         t_ua = a([t_us, t_u0], lambda: S.activation(T.ut[:, b1:b1 + 449:64], T.us_sb[:, e:32:4], COPY))
         t_ut = v([t_us, t_u0], lambda: V.tensor_copy(T.ut[:, b0:b0 + 449:64], T.us_sb[:, e:32:4]))
+    t_q = quant_x(3)
     t_uq = v([t_ut, t_ua], lambda: V.quantize_mx(T.uq[:], T.up[:], T.ut[:]))
     for i in (3, 2, 1, 0):
         if i < 3:
@@ -122,7 +138,10 @@ def rank_program(g, core, T, topo):
                 call()
             else:
                 t_sm = op("p", [], call, "px")
-    zero_v(ZV[1], 0)
+    zero_v(ZV[1])
+    v([], lambda: V.memset(T.rt[:, 0:32], 0.0))
+    v([], lambda: V.memset(T.rt4[:, 0:32], 0.0))
+    t_f2 = v([], lambda: V.memset(T.rr[:, 159:1024:32], 0.0))
     t_own = v([t_sm], lambda: V.tensor_copy(T.sc[:, 32 * u:32 * u + 32], T.ps0[:, 0:32]))
 
     def send(dst, view, rsem, lsem):
@@ -145,18 +164,9 @@ def rank_program(g, core, T, topo):
     for h in ZA[1:]:
         for k in range(2):
             zero_a(h, k)
-    t_dc = a([t_dl], lambda: S.activation(T.dc[:], T.dl[:], IDENT, bias=0.5 - CAP * u))
-    zero_v(ZV[1], 1)
+    t_dc = a([t_dl], lambda: S.activation(T.dc[:], T.dl[:], IDENT, bias=-0.5))
     for h in ZV[2:]:
         zero_v(h)
-    c2 = v([t_ip], lambda: V.tensor_scalar(T.ial[:], T.ip[:], 15, 2, A.bitwise_and, A.arith_shift_right))
-    c3 = v([], lambda: V.tensor_scalar(T.it3[:], T.ip[:], 3, None, A.bitwise_and))
-    v([], lambda: V.memset(T.ll[:, 0:240], 2048.0))
-    c6 = v([c2], lambda: V.tensor_copy(T.alf[:], T.ial[:]))
-    c7 = v([c3], lambda: V.tensor_copy(T.t3f[:], T.it3[:]))
-    v([], lambda: V.memset(T.rt[:, 0:32], 0.0))
-    t_f2 = v([], lambda: V.memset(T.rr[:, 159:1024:32], 0.0))
-    t_kk = v([c6, t_ki], lambda: V.tensor_scalar(T.kk[:], T.ki[:], T.alf[:], 4096.0, A.is_lt, A.mult))
     t_w = {}
     for h in WORD:
         t_w[h // 2] = dma("s", [t_z[h]], T.wm[16 * h:16 * h + 16, 1024 * h:1024 * h + 1024], T.w[16 * h:16 * h + 16, :],
@@ -166,72 +176,102 @@ def rank_program(g, core, T, topo):
     def quant_w(i):
         t_wq[i] = v([t_w[i]], lambda: V.quantize_mx(T.wq[:, 512 * i:512 * i + 512], T.wp[:, 512 * i:512 * i + 512],
                                                     T.wm[:, 2048 * i:2048 * i + 2048]))
-    for i in QEARLY:
+    c2 = v([t_ip], lambda: V.tensor_scalar(T.ial[:], T.ip[:], 15, 2, A.bitwise_and, A.arith_shift_right))
+    c3 = v([], lambda: V.tensor_scalar(T.it3[:], T.ip[:], 3, None, A.bitwise_and))
+    v([], lambda: V.memset(T.ll[:, 0:240], 2048.0))
+    c6 = v([c2], lambda: V.tensor_copy(T.alf[:], T.ial[:]))
+    c7 = v([c3], lambda: V.tensor_copy(T.t3f[:], T.it3[:]))
+    quant_w(QEARLY[0])
+    t_kk = v([c6, t_ki], lambda: V.tensor_scalar(T.kk[:], T.ki[:], T.alf[:], 4096.0, A.is_lt, A.mult))
+    for i in QEARLY[1:]:
         quant_w(i)
 
-    need("v", [("s%d" % s, n_in[s]) for s in senders])
-    m1 = v([t_own], lambda: V.tensor_tensor(T.m64[:], T.sc[:, 0:64], T.sc[:, 64:128], A.max))
-    v([], lambda: V.tensor_tensor(T.ab[:, 64:128], T.sc[:, 64:128], T.sc[:, 0:64], A.is_gt))
-    v([m1], lambda: V.tensor_tensor(T.cc[:, 0:32], T.m64[:, 32:64], T.m64[:, 0:32], A.is_le))
-    m2 = v([], lambda: V.tensor_tensor(T.cc[:, 32:64], T.m64[:, 32:64], T.m64[:, 0:32], A.is_gt))
-    m0 = v([], lambda: V.tensor_tensor(T.ab[:, 0:64], T.sc[:, 64:128], T.sc[:, 0:64], A.is_le))
-    v([m2], lambda: V.tensor_tensor(T.ww[:, 64:128], T.ab[:, 64:128], T.cc[:], A.mult))
-    t_ww = v([m0], lambda: V.tensor_tensor(T.ww[:, 0:64], T.ab[:, 0:64], T.cc[:], A.mult))
-    win = T.ww[:, 32 * u:32 * u + 32]
-    t1 = v([t_ww, t_gc], lambda: V.tensor_tensor_scan(T.rr[:, 0:128], T.m32[:], T.ww[:], 0.0, A.mult, A.add))
-    b1 = v([], lambda: V.tensor_tensor(T.w2[:], win, T.dl[:], A.mult))
-    t2 = v([t1, t_f2], lambda: V.transpose(T.rt[:, 32:64], T.rr[:, 31:1024:32]))
-    b2 = v([b1, t_dc], lambda: V.tensor_tensor(T.u2[:], T.dc[:], T.w2[:], A.subtract))
-    t3 = v([t2], lambda: V.tensor_tensor_scan(T.ea[:], T.rt[:, 31:63], T.lim[:], 1e6, A.add, A.min))
-    b3 = v([b2], lambda: V.tensor_tensor(T.ta[:], T.u2[:], T.rr[:, 32 * u:32 * u + 32], A.add))
+    def beats(out, s):
+        return tt([t_own, ("s%d" % s, n_in[s])], out[:], T.sc[:, 32 * u:32 * u + 32], T.sc[:, 32 * SLOT[s]:32 * SLOT[s] + 32],
+                  A.is_gt if s < r else A.is_ge)
+    lo64, hi64 = T.sc[:, 0:64], T.sc[:, 64:128]
+    beats(T.c1, senders[0])
+    t = beats(T.c2, senders[1])
+    t = tt([t], T.c12[:], T.c1[:], T.c2[:], A.mult)
+    t = beats(T.c3, senders[2])
+    m1 = tt([], T.m64[:], lo64, hi64, A.max)
+    tt([], T.ab[:, 64:128], hi64, lo64, A.is_gt)
+    t_win = tt([t], T.win[:], T.c12[:], T.c3[:], A.mult)
+    tt([m1], T.cc[:, 0:32], T.m64[:, 32:64], T.m64[:, 0:32], A.is_le)
+    tt([], T.cc[:, 32:64], T.m64[:, 32:64], T.m64[:, 0:32], A.is_gt)
+    t1 = v([t_win, t_gc], lambda: V.tensor_tensor_scan(T.ra[:], T.m32[:, 0:32], T.win[:], 0.0, A.min, A.add))
+    b1 = tt([], T.w2[:], T.win[:], T.dl[:], A.mult)
+    m2 = tt([], T.ab[:, 0:64], hi64, lo64, A.is_le)
+    t2 = v([t1], lambda: V.transpose(T.rt[:, 32:64], T.ra[:]))
+    b2 = tt([b1, t_dc], T.u2[:], T.dc[:], T.w2[:], A.subtract)
+    tt([], T.ww[:, 64:128], T.ab[:, 64:128], T.cc[:], A.mult)
+    t3 = v([t2], lambda: V.tensor_tensor_scan(T.ea[:], T.rt[:, 31:63], T.lim[:], 0.0, A.add, A.min))
+    b3 = tt([b2], T.ta[:], T.u2[:], T.ra[:], A.add)
+    m3 = tt([m2], T.ww[:, 0:64], T.ab[:, 0:64], T.cc[:], A.mult)
     t4 = v([t3], lambda: V.transpose(T.et[:], T.ea[:]))
-    for s in range(NR):
-        c = 32 * s
-        tp = a([t4], lambda: S.activation(T.p4[:, c:c + 32], T.rr[:, c:c + 32], IDENT, bias=T.et[:, s:s + 1]))
-    q1 = v([], lambda: V.tensor_tensor(T.q1[:], T.ww[:, 64:96], T.ww[:, 96:128], A.add))
-    t6 = v([t4, b3], lambda: V.tensor_scalar(T.ou[:], T.ta[:], T.et[:, u:u + 1], 1.25, A.add, A.mult))
-    q2 = v([q1], lambda: V.tensor_tensor(T.q2[:], T.q1[:], T.cc[:, 32:64], A.add))
-    t7 = v([t6], lambda: V.tensor_copy(T.ll[:].indirect(T.ou[:]), T.vi[:]))
-    t_wn = v([q2], lambda: V.tensor_tensor(T.wnt[:], T.q2[:], T.cc[:, 32:64], A.add))
+    q1 = tt([], T.q1[:], T.ww[:, 64:96], T.ww[:, 96:128], A.add)
+    n1 = v([m3], lambda: V.tensor_tensor_scan(T.rr[:, 0:128], T.m32[:], T.ww[:], 0.0, A.min, A.add))
+    t6 = v([t4, b3], lambda: V.tensor_scalar(T.ou[:], T.ta[:], T.et[:, 31:32], 1.25, A.add, A.mult))
+    q2 = tt([q1], T.q2[:], T.q1[:], T.cc[:, 32:64], A.add)
+    n2 = v([n1, t_f2], lambda: V.transpose(T.rt4[:, 32:64], T.rr[:, 31:1024:32]))
+    t7 = v([t6, t_vi], lambda: V.tensor_copy(T.ll[:].indirect(T.ou[:]), T.vi[:]))
+    t_wn = tt([q2], T.wnt[:], T.q2[:], T.cc[:, 32:64], A.add)
+    n3 = v([n2], lambda: V.tensor_tensor_scan(T.e4[:], T.rt4[:, 31:63], T.lim[:], 0.0, A.add, A.min))
     t8 = v([t7, t_kk], lambda: V.tensor_tensor_scan(T.sl5[:], T.ll[:, 0:240], T.kk[:], 4096.0, A.min, A.max))
-    v([tp], lambda: V.tensor_tensor(T.pm[:, 0:64], T.p4[:, 0:64], T.ww[:, 0:64], A.mult))
+    n4 = v([n3], lambda: V.transpose(T.et4[:], T.e4[:]))
     t9 = v([t8, c7], lambda: V.tensor_scalar(T.offa[:], T.sl5[:, 4:240:5], T.t3f[:], None, A.add))
     t10 = a([t9], lambda: S.activation(T.cb[:, 384:768], T.xb[:].indirect(T.offa[:, 24:48]), COPY))
-    t = v([], lambda: V.tensor_tensor(T.pm[:, 64:128], T.p4[:, 64:128], T.ww[:, 64:128], A.mult))
+
+    def column(s):
+        return v([n4], lambda: V.tensor_scalar(T.p4[:, 32 * s:32 * s + 32], T.rr[:, 32 * s:32 * s + 32], T.et4[:, s:s + 1],
+                                               float(CAP * s - 1), A.add, A.add))
+    column(0)
+    column(1)
     t11 = v([t9], lambda: V.tensor_copy(T.cb[:, 0:384], T.xb[:].indirect(T.offa[:, 0:24])))
-    t = v([t], lambda: V.tensor_tensor(T.ph[:], T.pm[:, 0:64], T.pm[:, 64:128], A.add))
+    column(2)
+    p4 = column(3)
     lo = CAP * u
     t_c = v([t10, t11], lambda: V.quantize_mx(T.lq[:, lo:lo + CAP], T.lp[:, lo:lo + CAP], T.cb[:]))
     need("g", [t_c])
     for n, d in enumerate(peers):
         send(d, T.lq[:, lo:lo + CAP].bitcast(dt.uint8), "c%d" % r, "cl%d" % n)
         send(d, T.lp[:, lo:lo + CAP], "c%d" % r, "cl%d" % n)
-
-    for k in range(4):
-        c = 16 * (k // 2)
-        td = v([t], lambda: V.tensor_tensor(T.dd[:, 16 * k:16 * k + 16], T.ph[:, c:c + 16], T.ph[:, 32 + c:48 + c], A.add))
-    for i in range(4):
-        if i not in QEARLY:
-            quant_w(i)
-    t = v([td], lambda: V.transpose(T.xf[:], T.dd[:]))
-    for k in range(2):
-        t_xu = v([t], lambda: V.tensor_copy(T.xu[:, k:64:2], T.xf[:, 32 * k:32 * k + 32]))
-    t_ob = {}
-    for b in (3, 0, 1, 2):
-        for d in range(4):
-            t_ob[b] = dma("s", [t_xu, ("cl0", cnt["cl0"])], T.offb[32 * d:32 * d + 32, 64 * b:64 * b + 64], T.xu[32 * b:32 * b + 32, :], "ob%d" % b)
     dma("g", [t_wn], T.wn[:], T.wnt[:], "wn")
+
+    t_ob = {}
+
+    def big_lists():
+        for k in range(2):
+            t = tt([p4], T.pm[:, 64 * k:64 * k + 64], T.p4[:, 64 * k:64 * k + 64], T.ww[:, 64 * k:64 * k + 64], A.mult)
+            yield
+        t = tt([t], T.ph[:], T.pm[:, 0:64], T.pm[:, 64:128], A.add)
+        yield
+        for k in range(4):
+            c = 16 * (k // 2)
+            td = tt([t], T.dd[:, 16 * k:16 * k + 16], T.ph[:, c:c + 16], T.ph[:, 32 + c:48 + c], A.add)
+            yield
+        t = v([td], lambda: V.transpose(T.xf[:], T.dd[:]))
+        yield
+        v([t], lambda: V.tensor_copy(T.xu[:, 0:64:2], T.xf[:, 0:32]))
+        yield
+        t = v([], lambda: V.tensor_copy(T.xu[:, 1:64:2], T.xf[:, 32:64]))
+        for b in (3, 0, 1, 2):
+            for d in range(4):
+                t_ob[b] = dma("s", [t, ("cl0", cnt["cl0"])], T.offb[32 * d:32 * d + 32, 64 * b:64 * b + 64],
+                              T.xu[32 * b:32 * b + 32, :], "ob%d" % b)
+        yield
+    lists = big_lists()
 
     banks = {"v": [T.ps0, T.ps1, T.ps2, T.ps3], "a": [T.ps4, T.ps5, T.ps6, T.ps7]}
     hist = {"v": [], "a": []}
     ready = {}
 
-    def product(s, h, o, e, deps):
+    def product(s, h, o, e):
         n = len(hist[e])
         bank = banks[e][n % 4]
         old = [hist[e][n - 4]] if n >= 4 else [t_own]
         w0, c0 = 256 * h + 128 * o, CAP * SLOT[s]
-        tk = op("p", deps + old + [t_wq[h // 2]], lambda: g.tensor.matmul_mx(
+        tk = op("p", [t_c if s == r else ("c%d" % s, 2 * n_in[s])] + old + [t_wq[h // 2]], lambda: g.tensor.matmul_mx(
             bank[:, 0:CAP], T.wq[:, w0:w0 + 128], T.wp[:, w0:w0 + 128], T.lq[:, c0:c0 + CAP], T.lp[:, c0:c0 + CAP],
             True, True), "p" + e)
         d0 = RW * (2 * h + o) + c0
@@ -242,72 +282,49 @@ def rank_program(g, core, T, topo):
         hist[e].append(c)
         ready[(s, h, o)] = c
 
-    def window(h, o):
-        d0 = RW * (2 * h + o)
-        return T.rw[:, d0:d0 + RW]
-
-    def rdeps(h, o):
-        return [ready[(s, h, o)] for s in range(NR)] + [t_ob[h // 2]]
-
-    jobs = [(h, o) for h in range(8) for o in range(2)]
-    for s, who in zip([r] + senders[:2], COPIES):
-        for (h, o), e in zip(jobs, who):
-            product(s, h, o, e, [t_c] if s == r else [("c%d" % s, 2 * n_in[s])])
-    s = senders[2]
-    dep = [("c%d" % s, 2 * n_in[s])]
-
     def add_dma(deps, out, in_, sem):
         return op("g", deps, lambda: g.dma_start(out, in_, accum_op=A.add), sem, 16)
 
     got = {}
     cur = {}
-    left = [sum(1 for st in TAIL if st[0] == "s" and int(st[2]) == o and st[3:] != "h") for o in range(2)]
+    left = [sum(1 for st in PLAN if st[0] == "s" and int(st[2]) == o and st[3:] != "h") for o in range(2)]
     done = [0, 0]
-    for step in TAIL:
-        h, o = int(step[1]), int(step[2])
-        halves = {"": (0, 1), "l": (0,), "h": (1,)}[step[3:]]
-        c0, c1 = 256 * halves[0], 256 * halves[-1] + 256
-        picked = window(h, o).indirect(T.offb[:, 32 * h + c0 // 16:32 * h + c1 // 16])
-        if step[0] == "g":
-            out = T[GBUF[(h, o)]]
-            got[(h, o)] = a(rdeps(h, o), lambda: S.activation(out[:, c0:c1], picked, COPY))
-            if h == 7:
-                for k in halves:
-                    cur[(o, k)] = (out, got[(h, o)])
-            if (5, 0) in got and (6, 0) in got and "g" not in cur:
-                cur["g"] = add_dma([got[(5, 0)], got[(6, 0)]], T.g6[:], T.g5[:], "ga")
-                if Y0 == "g":
-                    t_y0 = dma("s", [cur["g"]], T.y[:, 0:512], T.g6[:], "y0")
-        elif step[0] == "s":
+    extra = [int(st[1]) for st in PLAN if st[0] == "g" and st[1] != "7"]
+    for step in PLAN:
+        if step == "L":
+            next(lists)
+        elif step == "Q":
+            quant_w(3)
+        elif step[0] in "va":
+            product(([r] + senders)[int(step[1])], int(step[2]), int(step[3]), step[0])
+        else:
+            h, o = int(step[1]), int(step[2])
+            halves = {"": (0, 1), "l": (0,), "h": (1,)}[step[3:]]
+            c0, c1 = 256 * halves[0], 256 * halves[-1] + 256
+            d0 = RW * (2 * h + o)
+            picked = T.rw[:, d0:d0 + RW].indirect(T.offb[:, 32 * h + c0 // 16:32 * h + c1 // 16])
+            deps = [ready[(s, h, o)] for s in range(NR)] + [t_ob[h // 2]]
+            if step[0] == "g":
+                out = T[GBUF[(h, o)]]
+                got[(h, o)] = a(deps, lambda: S.activation(out[:, c0:c1], picked, COPY))
+                if h == 7:
+                    for k in halves:
+                        cur[(o, k)] = (out, got[(h, o)])
+                elif h == extra[-1]:
+                    t_g = got[(h, 0)] if len(extra) == 1 else add_dma([got[(5, 0)], got[(6, 0)]], T.g6[:], T.g5[:], "ga")
+                continue
             if step[3:] != "h":
                 done[o] += 1
             out = T["ac%d" % (2 * o + done[o] % 2)]
-            src = cur[(o, halves[0])][0]
-            tk = v([cur[(o, k)][1] for k in halves] + rdeps(h, o), lambda: V.tensor_tensor(out[:, c0:c1], picked, src[:, c0:c1], A.add))
+            tk = tt([cur[(o, k)][1] for k in halves] + deps, out[:, c0:c1], picked, cur[(o, halves[0])][0][:, c0:c1], A.add)
             for k in halves:
                 cur[(o, k)] = (out, tk)
-            if done[o] == left[o]:
-                if o == 1:
-                    dma(("s", "a")[halves[0]], [tk], T.y[:, 512 + c0:512 + c1], out[:, c0:c1], "y%d" % (1 + halves[0]))
-                elif halves == (0,):
-                    pass
-                elif Y0 == "g":
-                    add_dma([tk, t_y0], T.y[:, 0:512], out[:], "gb")
-                else:
-                    t_y0 = dma("s", [tk], T.y[:, 0:512], out[:], "y0")
-                    add_dma([cur["g"], t_y0], T.y[:, 0:512], T.g6[:], "gb")
-        else:
-            product(s, h, o, step[0], dep)
+            if done[o] == left[o] and o == 1:
+                dma(("s", "a")[halves[0]], [tk], T.y[:, 512 + c0:512 + c1], out[:, c0:c1], "y%d" % (1 + halves[0]))
+            elif done[o] == left[o] and halves != (0,):
+                t_y0 = dma("s", [tk], T.y[:, 0:512], out[:], "y0")
+                y0 = out
+    if extra:
+        add_dma([t_g, t_y0], T.y[:, 0:512], T.g6[:], "gb")
 
     need("g", sorted(cnt.items()))
-
-
-ZA = (0, 1, 4, 6)
-ZV = (2, 3, 5, 7)
-WORD = (0, 2, 1, 4, 3, 5, 6, 7)
-QEARLY = (0, 1, 2)
-COPIES = ("aavavavavavavava", "vavavavavavavava", "vavavavavavavava")
-GBUF = {(7, 0): "g0", (7, 1): "g1", (6, 0): "g6", (5, 0): "g5"}
-Y0 = "v"
-TAIL = ("a70 v00 a60 v10 v20 g70l g70h a50 g60 a30 a40 g50 a71 a01 g71 a11 a21 a31 a41 a51 a61".split()
-        + ["s%d%d%s" % (h, o, k) for o, n in ((0, 5), (1, 7)) for h in range(n) for k in "lh"])

@@ -3,50 +3,84 @@ from concourse.mybir import dt, AluOpType, ActivationFunctionType
 
 CAP = 192
 NR = 4
-RW = NR * CAP
-LW = 5632
+NL = 6
+NE = 4
+EX = 80
+WID = CAP + EX
+XE = 4 * 576
+OWN = 3 * CAP
+RW = OWN + 512
+LW = 6016
 SLOT = (0, 2, 1, 3)
 F, I32, U16, BF, X4, U8 = "float32", "int32", "uint16", "bfloat16", "float8_e4m3fn_x4", "uint8"
 _sb = {
-    "us_sb": (32, BF), "ut": (4 * 288, BF), "uq": (288, X4), "up": (288, U8),
-    "xb": (4 * 608, BF), "xq": (608, X4), "xp": (608, U8),
-    "zt": (512, BF), "wm": (8192, BF), "wq": (2048, X4), "wp": (2048, U8),
-    "cb": (4 * CAP, BF), "lq": (RW, X4), "lp": (RW, U8), "sc": (128, F),
-    "ip": (1, I32), "ial": (1, I32), "it3": (1, I32), "alf": (1, F), "t3f": (1, F),
-    "vi": (512, F), "dl": (32, F), "dc": (32, F), "ki": (240, F), "kk": (240, F), "m32": (128, F), "lim": (32, F),
+    "us_sb": (32, BF), "ut": (4 * 142, BF), "uq": (142, X4), "up": (142, U8), "sh": (64, F),
+    "xb": (XE + 4 * EX + 16, BF), "xq": (576, X4), "xp": (576, U8),
+    "zt": (512, BF), "wm": (7 * 1024, BF), "wq": (2560, X4), "wp": (2560, U8),
+    "cb": (4 * (CAP + 128), BF), "lq": (3 * WID + CAP + 128, X4), "lp": (3 * WID + CAP + 128, U8), "sc": (128, F),
+    "pre": (192, F), "col": (192, F), "ia": (32, F),
+    "vi": (512, F), "vt": (512, F), "dl": (32, F), "dc": (32, F), "ki": (240, F), "kk": (240, F), "m32": (128, F), "lim": (32, F),
     "c1": (32, F), "c2": (32, F), "c3": (32, F), "c12": (32, F), "win": (32, F), "ra": (32, F), "rt": (64, F), "ea": (32, F),
-    "et": (32, F), "w2": (32, F), "u2": (32, F), "ta": (32, F), "ou": (32, U16), "ll": (LW, F), "sl5": (240, F), "offa": (48, U16),
+    "et": (32, F), "w2": (32, F), "u2": (32, F), "ta": (32, F), "ou": (32, U16), "ll": (LW, F), "sl5": (240, F),
+    "offa": (WID // 4, U16), "le": (100, F), "se": (100, F),
     "ab": (128, F), "m64": (64, F), "cc": (64, F), "ww": (128, F), "rr": (1024, F), "rt4": (64, F), "e4": (32, F), "et4": (32, F),
-    "p4": (128, F), "pm": (128, F), "ph": (64, F), "dd": (64, F), "xf": (64, F), "xu": (64, U16), "offb": (256, U16),
+    "p4": (128, F), "pm": (128, F), "ph": (64, F), "dd": (64, F), "xf": (64, F), "xg": (32 * NL, F), "offb": (32 * NL, U16),
     "q1": (32, F), "q2": (32, F), "wnt": (32, F),
-    "rw": (16 * RW, F), "g0": (512, F), "g1": (512, F), "g5": (512, F), "g6": (512, F), "ac0": (512, F),
-    "ac1": (512, F), "ac2": (512, F), "ac3": (512, F),
+    "rw": (2 * NL * RW, F), "aca": (512, F), "acb": (512, F), "acc": (512, F), "acd": (512, F), "ace": (512, F), "acf": (512, F),
 }
 SCRATCH = {k: ("sbuf", [128, n], d) for k, (n, d) in _sb.items()}
 for _k in range(8):
     SCRATCH["ps%d" % _k] = ("psum", [128, 512], F)
-SEMAPHORES = (["v", "a", "pv", "pa", "px", "gi", "us", "wn", "ga", "gb", "y0", "y1", "y2", "sloc"]
-              + [n + str(i) for n in ("x", "w", "s", "c", "ob", "cl") for i in range(4)])
+SEMAPHORES = (["v", "a", "pv", "pa", "px", "pb", "gi", "us", "xe", "zd", "wn", "sloc", "cl", "fed0", "fed1"]
+              + [n + str(i) for n in ("x", "s", "c", "e") for i in range(4)]
+              + ["w%d" % i for i in range(7)] + ["d%d" % i for i in range(1, 11)])
 
-ZA = (0, 1, 4, 6, 7)
-ZV = (2, 3, 5)
-WORD = (0, 2, 1, 3, 4, 5, 6, 7)
-QEARLY = (0, 1, 2)
-GBUF = {(7, 0): "g0", (7, 1): "g1", (6, 0): "g6", (5, 0): "g5"}
-_JOBS = ["%d%d" % (h, o) for h in range(8) for o in range(2)]
-_NEED = "70 00 10 60 20 50 30 40 71 01 11 21 31 41 51 61".split()
-PLAN = ("L L Q a000 a001 L a010 v011 L L L L a020 v021 L a030 v031 L L".split()
-        + [e + "0" + j for e, j in zip("va" * 4, _JOBS[8:])]
-        + [e + "1" + j for e, j in zip("va" * 8, _NEED)]
-        + [e + "2" + j for e, j in zip("va" * 8, _NEED[:9])]
-        + "a370 v300 a360 v310 g70l v320 g70h v330 a350 g60 a371 g50 a340 g71".split()
-        + ["a" + k + j for j in _NEED[9:] for k in "23"]
-        + ["s%d%d%s" % (h, o, k) for o, n in ((0, 5), (1, 7)) for h in range(n) for k in "lh"])
+BLK = {0: 1, 2: 2, 4: 3, 5: 4, 1: 5, 3: 6}
+VBLK = {3: 0, 0: 1, 1: 2, 2: 3}
+QUANT = ((0, 2), (1, 3), (4, 5))
+FIRST = {3: CAP, 0: CAP + EX, 1: CAP + 2 * EX, 2: CAP + 3 * EX}
+XLOAD = ((2, 4), (1, 2), (0, 1))
+RELAY = ()
+EARLY = "00 01 20 21 10 11 30 31".split()
+FILL = "LL LL L L LL L LL LL L LL LL -".split()
+WIDE = ()
+BORDER = ((1, 2, 0, 3), (3, 0, 1, 2))
+GS = 40
+PARTS = {"": (0, 512), "l": (0, 352), "h": (352, 512), "x": (0, 256), "y": (256, 512)}
+PLAN = """
+S0 S1 S2 T L L T Q3 L a040 a041 v050 L Q4 L T S310 a051 Q5 Q6
+a150 v100 a140 v110 L a130 v120 L a151 v101 L N a111 v121
+a250 v200 a240 v210 a230 v220 a251 v201
+v300 a350 v310 a340 v320 s00a/y s00a/x g50c +a330 +a351 +a301 *00 g40d Dcd s10a/y s10a/x a330 a351 a301 +a211 +a311
+*0123 s20a/y s20a/x g51b/l g51b/h s30a/y s30a/x vB10a vB20a vB00a vB30a Ya0 Yc0 a211 a311 a221 a321 *101
+s01b/l s01b/h a131 a231 a331 *12 s11b/l s11b/h a141 a241 a341 *13
+s21b/l s21b/h s31b/l s31b/h vB31b vB01b vB11b vB21b s41b/l Yb1/l s41b/h Zb1/h
+""".split()
 
 
 def rank_program(g, core, T, topo):
     r = T.rank_of(core)
+
+    def relay_of(c):
+        return [k for k in topo.cores_of(c) if topo.die(k) == topo.die(c) and T.rank_of(k) is None][0]
+
+    def views(n, lo, hi):
+        return T.lq[:, WID * n + lo:WID * n + hi].bitcast(dt.uint8), T.lp[:, WID * n + lo:WID * n + hi]
+
+    def send_all(ds, outs, view, rsem, lsem):
+        ids = [DstId(rid=topo.addr(d)[0], pnc=topo.addr(d)[1]) for d in ds]
+        g.remote_dma_fused([RemoteDMATransfer(dst_ids=ids, dma_engine_mask=topo.mask(core, ds[0]), remote_sem=T.sem[rsem],
+                                              srcs=[view], dsts=outs)], local_sem=T.sem[lsem])
+        return len(topo.engines(core, ds[0]))
+
+    def feed_mask(c, far):
+        return topo.mask(c, relay_of(c)) & ~topo.mask(c, far)
     if r is None:
+        for s, c in enumerate(T.cores):
+            if RELAY and relay_of(c) == core:
+                ds = [T.cores[(s + 1 + n) % NR] for n in RELAY]
+                g.wait_ge(T.sem["fed1"], bin(feed_mask(c, ds[0])).count("1"))
+                g.wait_ge(T.sem["cl"], send_all(ds, [views(n, 0, CAP)[1] for n in RELAY], views(3, 0, CAP)[1], "c%d" % s, "cl"))
         return
     A = AluOpType
     COPY = ActivationFunctionType.Copy
@@ -82,165 +116,221 @@ def rank_program(g, core, T, topo):
     def tt(deps, out, in0, in1, alu):
         return v(deps, lambda: V.tensor_tensor(out, in0, in1, alu))
 
-    peers = [(r + k) % NR for k in (1, 2, 3)]
+    peers = [T.cores[(r + k) % NR] for k in (1, 2, 3)]
     senders = [(r - k) % NR for k in (1, 2, 3)]
     u = SLOT[r]
 
     t_us = dma("s", [], T.us_sb[:], T.us[:, 0:32], "us")
     t_x = {}
-    for i, qn in ((3, "a"), (2, "s"), (1, "a"), (0, "s")):
-        t_x[i] = dma(qn, [], T.xb[:, 512 * i:512 * i + 512], T.x[:, 512 * i:512 * i + 512], "x%d" % i)
+    for n, (lo, hi) in enumerate(XLOAD):
+        t = dma("s", [], T.xb[:, 512 * lo:512 * hi], T.x[:, 512 * lo:512 * hi], "x%d" % n)
+        t_x.update({i: t for i in range(lo, hi)})
 
     def io(out, pattern, base, cm):
         return op("g", [], lambda: g.iota(out, pattern, base, cm, allow_small_or_imprecise_dtypes=True), "gi")
-    t_ip = io(T.ip[:], [[0, 1]], 0, 1)
+    io(T.pre[:, 0:32], [[0, 8], [1, 4]], 0, 0)
+    io(T.pre[:, 32:64], [[0, 2], [1, 4], [0, 4]], 0, 0)
+    io(T.pre[:, 64:96], [[0, 2], [-2048, 4], [0, 4]], 0, 0)
+    io(T.pre[:, 96:128], [[0, 2], [32, 16]], 0, 0)
+    io(T.pre[:, 128:160], [[0, 16], [-1, 2]], 1, 0)
+    t_pre = io(T.pre[:, 160:192], [[0, 16], [1, 2]], 0, 0)
+    t3f, alf = T.col[:, 0:1], T.col[:, 32:33]
     t_ki = io(T.ki[:], [[0, 48], [1, 5]], -1, 0)
+    io(T.ia[:], [[1, 32]], 1, 0)
     t_dl = io(T.dl[:], [[1, 32]], 200, 32)
-    io(T.lim[:], [[0, 2], [4096, 16]], 0, 0)
-    t_gc = io(T.m32[:], [[0, 4], [4096, 32]], 0, 0)
     t_vi = io(T.vi[:], [[4, 32], [128, 16]], 0, 0)
 
     t_zt = v([], lambda: V.memset(T.zt[:], 0.0))
     t_u0 = v([], lambda: V.memset(T.ut[:], 0.0))
-    t_f = v([], lambda: V.memset(T.xb[:, 2048:2432], 0.0))
+    t_f = v([], lambda: V.memset(T.xb[:, 2048:XE], 0.0))
+    v([], lambda: V.memset(T.et[96:128, 31:32], 0.0))
+    v([], lambda: V.memset(T.rt[:, 0:32], 0.0))
+    v([], lambda: V.memset(T.rt4[:, 0:32], 0.0))
+    t_f2 = v([], lambda: V.memset(T.rr[:, 159:1024:32], 0.0))
+    v([], lambda: V.memset(T.xb[:, XE + 4 * EX:XE + 4 * EX + 16], 0.0))
+    t_f3 = v([], lambda: V.memset(T.cb[:, 4 * WID:4 * (CAP + 128)], 0.0))
     t_z = {}
 
-    def zero_a(h, k):
-        c0 = 1024 * h + 512 * k
-        t_z[h] = a([t_zt], lambda: S.activation(T.wm[:, c0:c0 + 512], T.zt[:], COPY))
+    def zero_a(b, ks=(0, 1)):
+        for k in ks:
+            c0 = 1024 * b + 512 * k
+            t_z[b] = a([t_zt], lambda: S.activation(T.wm[:, c0:c0 + 512], T.zt[:], COPY))
 
-    def zero_v(h, k=None):
-        c0, n = (1024 * h, 1024) if k is None else (1024 * h + 512 * k, 512)
-        t_z[h] = v([], lambda: V.memset(T.wm[:, c0:c0 + n], 0.0))
+    def zero_v(b, k=None):
+        c0, n = (1024 * b, 1024) if k is None else (1024 * b + 512 * k, 512)
+        t_z[b] = v([], lambda: V.memset(T.wm[:, c0:c0 + n], 0.0))
 
     def quant_x(i):
-        lo, hi = 128 * i, (608 if i == 3 else 128 * i + 128)
+        lo, hi = 128 * i, (576 if i == 3 else 128 * i + 128)
         return v([t_x[i], t_f], lambda: V.quantize_mx(T.xq[:, lo:hi], T.xp[:, lo:hi], T.xb[:, 4 * lo:4 * hi]))
+    zero_a(BLK[2], (0,))
     for k in range(2):
-        zero_a(ZA[0], k)
-    zero_v(ZV[0])
+        c0 = 1024 * BLK[5] + 512 * k
+        t_z[BLK[5]] = dma("s", [t_zt], T.wm[:, c0:c0 + 512], T.zt[:], "zd")
 
     for e in range(4):
-        b0, b1 = 4 * 15 + e, 4 * (144 + 16) + e
+        b0, b1 = 4 * 14 + e, 4 * 15 + e
         t_ua = a([t_us, t_u0], lambda: S.activation(T.ut[:, b1:b1 + 449:64], T.us_sb[:, e:32:4], COPY))
         t_ut = v([t_us, t_u0], lambda: V.tensor_copy(T.ut[:, b0:b0 + 449:64], T.us_sb[:, e:32:4]))
-    t_q = quant_x(3)
+    zero_a(BLK[2], (1,))
+    zero_v(BLK[0], 0)
     t_uq = v([t_ut, t_ua], lambda: V.quantize_mx(T.uq[:], T.up[:], T.ut[:]))
     for i in (3, 2, 1, 0):
-        if i < 3:
-            t_q = quant_x(i)
+        t_q = quant_x(i)
+        if i == 2:
+            zero_v(BLK[0], 1)
         need("p", [t_uq, t_q])
-        for k in (4 * i + 3, 4 * i + 2, 4 * i + 1, 4 * i):
-            st = 15 - k if k % 2 else 144 + 16 - k
+        if i == 1:
+            t_col = v([t_pre], lambda: V.transpose(T.col[:], T.pre[:]))
+        for k in (2 * i + 1, 2 * i):
+            st = 14 - 2 * k
             call = lambda: g.tensor.matmul_mx(T.ps0[:, 0:128], T.uq[:, st:st + 128], T.up[:, st:st + 128],
-                                              T.xq[:, 32 * k:32 * k + 128], T.xp[:, 32 * k:32 * k + 128], k == 15, k == 0)
+                                              T.xq[:, 64 * k:64 * k + 128], T.xp[:, 64 * k:64 * k + 128], k == 7, k == 0)
             if k:
                 call()
             else:
                 t_sm = op("p", [], call, "px")
-    zero_v(ZV[1])
-    v([], lambda: V.memset(T.rt[:, 0:32], 0.0))
-    v([], lambda: V.memset(T.rt4[:, 0:32], 0.0))
-    t_f2 = v([], lambda: V.memset(T.rr[:, 159:1024:32], 0.0))
-    t_own = v([t_sm], lambda: V.tensor_copy(T.sc[:, 32 * u:32 * u + 32], T.ps0[:, 0:32]))
-
-    def send(dst, view, rsem, lsem):
-        d = T.cores[dst]
-        rid, pid, _se = topo.addr(d)
-        g.remote_dma(view, view, T.sem[rsem], T.sem[lsem], pid, rid, topo.mask(core, d))
-        cnt[lsem] = cnt.get(lsem, 0) + len(topo.engines(core, d))
-
-    def send_all(view, rsem, lsem):
-        ds = [T.cores[d] for d in peers]
-        ids = [DstId(rid=topo.addr(d)[0], pnc=topo.addr(d)[1]) for d in ds]
-        g.remote_dma_fused([RemoteDMATransfer(dst_ids=ids, dma_engine_mask=topo.mask(core, ds[0]), remote_sem=T.sem[rsem],
-                                              srcs=[view], dsts=[view] * 3)], local_sem=T.sem[lsem])
-        cnt[lsem] = cnt.get(lsem, 0) + len(topo.engines(core, ds[0]))
-
+    zero_v(BLK[4], 0)
+    mine = T.sc[:, 32 * u:32 * u + 32]
+    t = tt([t_sm, t_col], T.sh[:], T.ps0[:, 0:64], T.col[:, 128:192], A.mult)
+    zero_v(BLK[4], 1)
+    t_own = tt([t], mine, T.sh[:, 0:32], T.sh[:, 32:64], A.add)
     need("g", [t_own])
-    send_all(T.sc[:, 32 * u:32 * u + 32], "s%d" % r, "sloc")
+    t_sent = ("sloc", send_all(peers, [mine] * 3, mine, "s%d" % r, "sloc"))
+    cnt["sloc"] = t_sent[1]
     n_in = {s: len(topo.engines(T.cores[s], core)) for s in senders}
+    t_vt = io(T.vt[:], [[16, 8], [4 + 2048, 4], [128, 16]], 0, 0)
+    io(T.lim[:], [[0, 2], [4096, 16]], 0, 0)
+    t_gc = io(T.m32[:], [[0, 4], [4096, 32]], 0, 0)
+    t_ll = io(T.ll[:, 0:640], [[0, 640]], 2048, 0)
 
-    for h in ZA[1:]:
-        for k in range(2):
-            zero_a(h, k)
-    t_dc = a([t_dl], lambda: S.activation(T.dc[:], T.dl[:], IDENT, bias=-0.5))
-    for h in ZV[2:]:
-        zero_v(h)
+    zero_a(BLK[1])
+    zero_a(BLK[3])
     t_w = {}
-    for h in WORD:
-        t_w[h // 2] = dma("s", [t_z[h]], T.wm[16 * h:16 * h + 16, 1024 * h:1024 * h + 1024], T.w[16 * h:16 * h + 16, :],
-                          "w%d" % (h // 2))
     t_wq = {}
+    wcol = {}
+
+    def load_w(i):
+        for h in QUANT[i]:
+            c0 = 1024 * BLK[h]
+            t_w[i] = dma("s", [t_z[BLK[h]]], T.wm[16 * h:16 * h + 16, c0:c0 + 1024], T.w[16 * h:16 * h + 16, :], "w%d" % i)
+
+    def load_v(b, deps):
+        c0, i = 1024 * VBLK[b], 3 + VBLK[b]
+        t_w[i] = dma("s", deps, T.wm[32 * b:32 * b + 32, c0:c0 + 1024], T.w[96:128, :], "w%d" % i)
 
     def quant_w(i):
-        t_wq[i] = v([t_w[i]], lambda: V.quantize_mx(T.wq[:, 512 * i:512 * i + 512], T.wp[:, 512 * i:512 * i + 512],
-                                                    T.wm[:, 2048 * i:2048 * i + 2048]))
-    c2 = v([t_ip], lambda: V.tensor_scalar(T.ial[:], T.ip[:], 15, 2, A.bitwise_and, A.arith_shift_right))
-    c3 = v([], lambda: V.tensor_scalar(T.it3[:], T.ip[:], 3, None, A.bitwise_and))
-    v([], lambda: V.memset(T.ll[:, 0:240], 2048.0))
-    c6 = v([c2], lambda: V.tensor_copy(T.alf[:], T.ial[:]))
-    c7 = v([c3], lambda: V.tensor_copy(T.t3f[:], T.it3[:]))
-    quant_w(QEARLY[0])
-    t_kk = v([c6, t_ki], lambda: V.tensor_scalar(T.kk[:], T.ki[:], T.alf[:], 4096.0, A.is_lt, A.mult))
-    for i in QEARLY[1:]:
-        quant_w(i)
+        keys = QUANT[i] if i < 3 else [("v", b) for b in VBLK if VBLK[b] == i - 3]
+        c0, q0, n = (1024 * BLK[keys[0]], 512 * i, 512) if i < 3 else (1024 * (i - 3), 768 + 256 * i, 256)
+        t = v([t_w[i]], lambda: V.quantize_mx(T.wq[:, q0:q0 + n], T.wp[:, q0:q0 + n], T.wm[:, c0:c0 + 4 * n]))
+        for j, k in enumerate(keys):
+            t_wq[k] = t
+            wcol[k] = q0 + 256 * j
+    load_w(0)
+    load_w(1)
+    load_w(2)
+    quant_w(0)
+    for b in FIRST:
+        t_xe = dma("s", [t_sent], T.xb[32 * b:32 * b + 32, XE:XE + 4 * EX], T.x[96:128, 4 * FIRST[b]:4 * FIRST[b] + 4 * EX], "xe")
+    t_kk = v([t_col, t_ki], lambda: V.tensor_scalar(T.kk[:], T.ki[:], alf, 8192.0, A.is_lt, A.mult))
+    v([t_dl], lambda: V.tensor_scalar(T.ra[96:128, :], T.ia[96:128, :], T.col[96:128, 96:97], None, A.add))
+    if NE:
+        v([], lambda: V.tensor_scalar(T.p4[0:16 * NE, 32 * u:32 * u + 32], T.ia[0:16 * NE, :], T.col[0:16 * NE, 96:97], OWN - 1.0,
+                                      A.add, A.add))
+    quant_w(1)
+    quant_w(2)
+    t_dc = a([t_dl], lambda: S.activation(T.dc[:], T.dl[:], IDENT, bias=-0.5))
 
-    def beats(out, s):
-        return tt([t_own, ("s%d" % s, n_in[s])], out[:], T.sc[:, 32 * u:32 * u + 32], T.sc[:, 32 * SLOT[s]:32 * SLOT[s] + 32],
-                  A.is_gt if s < r else A.is_ge)
+    banks = {"v": [T.ps0, T.ps1, T.ps2, T.ps3], "a": [T.ps4, T.ps5, T.ps6, T.ps7]}
+    hist = {"v": [], "a": []}
+    ready = {}
+
+    def copy(e, deps, out, in_):
+        if e == "v":
+            return v(deps, lambda: V.tensor_copy(out, in_))
+        return a(deps, lambda: S.activation(out, in_, COPY))
+
+    ahead = {}
+
+    def product(name, e, key, o, moving, out):
+        if name in ahead:
+            e, n, tk, bank = ahead.pop(name)
+            hist[e][n] = out(tk, bank)
+            return hist[e][n]
+        n = len(hist[e])
+        bank = banks[e][n % 4]
+        old = [hist[e][n - 4]] if n >= 4 else [t_own]
+        w0 = wcol[key] + 128 * o
+        for i, (deps, q, p, c0, c1) in enumerate(moving):
+            need("p", deps + old + [t_wq[key]])
+            call = lambda: g.tensor.matmul_mx(bank[:, 0:c1 - c0], T.wq[:, w0:w0 + 128], T.wp[:, w0:w0 + 128], q[:, c0:c1], p[:, c0:c1],
+                                              i == 0, i == len(moving) - 1)
+            if i < len(moving) - 1:
+                call()
+            else:
+                tk = op("p", [], call, "p" + e)
+        if out is None:
+            ahead[name] = (e, n, tk, bank)
+        hist[e].append(out and out(tk, bank))
+        return hist[e][n]
+
+    def early(job):
+        h, o = int(job[0]), int(job[1])
+        d0 = RW * (2 * h + o) + OWN
+        ready[(0, h, o)] = product(job, "a", h, o, [([t_q], T.xq, T.xp, 0, 512)],
+                                   lambda tk, bank: copy("a", [tk], T.rw[:, d0:d0 + 512], bank[:]))
+    zero_a(VBLK[3])
+    load_v(3, [t_z[VBLK[3]]])
+    for b in range(3):
+        load_v(b, [t_wq[2 * b]])
+    for job in EARLY[:2]:
+        early(job)
+    t_vb = a([t_vt, t_vi, t_col], lambda: S.activation(T.vi[96:128, :], T.vt[96:128, :], IDENT, bias=T.col[96:128, 64:65]))
+    for job in EARLY[2:]:
+        early(job)
+
+    t_ob = []
+    t_wn = []
     lo64, hi64 = T.sc[:, 0:64], T.sc[:, 64:128]
-    beats(T.c1, senders[0])
-    t = beats(T.c2, senders[1])
-    t = tt([t], T.c12[:], T.c1[:], T.c2[:], A.mult)
-    t = beats(T.c3, senders[2])
-    m1 = tt([], T.m64[:], lo64, hi64, A.max)
-    tt([], T.ab[:, 64:128], hi64, lo64, A.is_gt)
-    t_win = tt([t], T.win[:], T.c12[:], T.c3[:], A.mult)
-    tt([m1], T.cc[:, 0:32], T.m64[:, 32:64], T.m64[:, 0:32], A.is_le)
-    tt([], T.cc[:, 32:64], T.m64[:, 32:64], T.m64[:, 0:32], A.is_gt)
-    t1 = v([t_win, t_gc], lambda: V.tensor_tensor_scan(T.ra[:], T.m32[:, 0:32], T.win[:], 0.0, A.min, A.add))
-    b1 = tt([], T.w2[:], T.win[:], T.dl[:], A.mult)
-    m2 = tt([], T.ab[:, 0:64], hi64, lo64, A.is_le)
-    t2 = v([t1], lambda: V.transpose(T.rt[:, 32:64], T.ra[:]))
-    b2 = tt([b1, t_dc], T.u2[:], T.dc[:], T.w2[:], A.subtract)
-    tt([], T.ww[:, 64:128], T.ab[:, 64:128], T.cc[:], A.mult)
-    t3 = v([t2], lambda: V.tensor_tensor_scan(T.ea[:], T.rt[:, 31:63], T.lim[:], 0.0, A.add, A.min))
-    b3 = tt([b2], T.ta[:], T.u2[:], T.ra[:], A.add)
-    m3 = tt([m2], T.ww[:, 0:64], T.ab[:, 0:64], T.cc[:], A.mult)
-    t4 = v([t3], lambda: V.transpose(T.et[:], T.ea[:]))
-    q1 = tt([], T.q1[:], T.ww[:, 64:96], T.ww[:, 96:128], A.add)
-    n1 = v([m3], lambda: V.tensor_tensor_scan(T.rr[:, 0:128], T.m32[:], T.ww[:], 0.0, A.min, A.add))
-    t6 = v([t4, b3], lambda: V.tensor_scalar(T.ou[:], T.ta[:], T.et[:, 31:32], 1.25, A.add, A.mult))
-    q2 = tt([q1], T.q2[:], T.q1[:], T.cc[:, 32:64], A.add)
-    n2 = v([n1, t_f2], lambda: V.transpose(T.rt4[:, 32:64], T.rr[:, 31:1024:32]))
-    t7 = v([t6, t_vi], lambda: V.tensor_copy(T.ll[:].indirect(T.ou[:]), T.vi[:]))
-    t_wn = tt([q2], T.wnt[:], T.q2[:], T.cc[:, 32:64], A.add)
-    n3 = v([n2], lambda: V.tensor_tensor_scan(T.e4[:], T.rt4[:, 31:63], T.lim[:], 0.0, A.add, A.min))
-    t8 = v([t7, t_kk], lambda: V.tensor_tensor_scan(T.sl5[:], T.ll[:, 0:240], T.kk[:], 4096.0, A.min, A.max))
-    n4 = v([n3], lambda: V.transpose(T.et4[:], T.e4[:]))
-    t9 = v([t8, c7], lambda: V.tensor_scalar(T.offa[:], T.sl5[:, 4:240:5], T.t3f[:], None, A.add))
-    t10 = a([t9], lambda: S.activation(T.cb[:, 384:768], T.xb[:].indirect(T.offa[:, 24:48]), COPY))
 
-    def column(s):
-        return v([n4], lambda: V.tensor_scalar(T.p4[:, 32 * s:32 * s + 32], T.rr[:, 32 * s:32 * s + 32], T.et4[:, s:s + 1],
-                                               float(CAP * s - 1), A.add, A.add))
-    column(0)
-    column(1)
-    t11 = v([t9], lambda: V.tensor_copy(T.cb[:, 0:384], T.xb[:].indirect(T.offa[:, 0:24])))
-    column(2)
-    p4 = column(3)
-    lo = CAP * u
-    t_c = v([t10, t11], lambda: V.quantize_mx(T.lq[:, lo:lo + CAP], T.lp[:, lo:lo + CAP], T.cb[:]))
-    need("g", [t_c])
-    for n, d in enumerate(peers):
-        send(d, T.lq[:, lo:lo + CAP].bitcast(dt.uint8), "c%d" % r, "cl%d" % n)
-        send(d, T.lp[:, lo:lo + CAP], "c%d" % r, "cl%d" % n)
-    dma("g", [t_wn], T.wn[:], T.wnt[:], "wn")
-
-    t_ob = {}
+    def column(deps, s):
+        c0, p0 = 32 * SLOT[s], (16 * NE if s == r else 0)
+        base = OWN if s == r else CAP * senders.index(s)
+        return v(deps, lambda: V.tensor_scalar(T.p4[p0:128, c0:c0 + 32], T.rr[p0:128, c0:c0 + 32], T.et4[p0:128, SLOT[s]:SLOT[s] + 1],
+                                               float(base - 1), A.add, A.add))
 
     def big_lists():
+        m1 = tt([], T.m64[:], lo64, hi64, A.max)
+        yield
+        tt([], T.ab[:, 64:128], hi64, lo64, A.is_gt)
+        yield
+        tt([m1], T.cc[:, 0:32], T.m64[:, 32:64], T.m64[:, 0:32], A.is_le)
+        yield
+        t = tt([], T.cc[:, 32:64], T.m64[:, 32:64], T.m64[:, 0:32], A.is_gt)
+        yield
+        m2 = tt([], T.ab[:, 0:64], hi64, lo64, A.is_le)
+        yield
+        w1 = tt([t], T.ww[:, 64:128], T.ab[:, 64:128], T.cc[:], A.mult)
+        yield
+        m3 = tt([m2], T.ww[:, 0:64], T.ab[:, 0:64], T.cc[:], A.mult)
+        yield
+        q1 = tt([w1], T.q1[:], T.ww[:, 64:96], T.ww[:, 96:128], A.add)
+        yield
+        n1 = v([m3], lambda: V.tensor_tensor_scan(T.rr[:, 0:128], T.m32[:], T.ww[:], 0.0, A.min, A.add))
+        yield
+        q2 = tt([q1], T.q2[:], T.q1[:], T.cc[:, 32:64], A.add)
+        yield
+        t = v([n1, t_f2], lambda: V.transpose(T.rt4[:, 32:64], T.rr[:, 31:1024:32]))
+        yield
+        t_wn.append(tt([q2], T.wnt[:], T.q2[:], T.cc[:, 32:64], A.add))
+        yield
+        t = v([t], lambda: V.tensor_tensor_scan(T.e4[:], T.rt4[:, 31:63], T.lim[:], 0.0, A.add, A.min))
+        yield
+        n4 = v([t], lambda: V.transpose(T.et4[:], T.e4[:]))
+        yield
+        for s in range(NR):
+            p4 = column([n4], s)
+            yield
         for k in range(2):
             t = tt([p4], T.pm[:, 64 * k:64 * k + 64], T.p4[:, 64 * k:64 * k + 64], T.ww[:, 64 * k:64 * k + 64], A.mult)
             yield
@@ -249,82 +339,209 @@ def rank_program(g, core, T, topo):
         for k in range(4):
             c = 16 * (k // 2)
             td = tt([t], T.dd[:, 16 * k:16 * k + 16], T.ph[:, c:c + 16], T.ph[:, 32 + c:48 + c], A.add)
-            yield
+        yield
         t = v([td], lambda: V.transpose(T.xf[:], T.dd[:]))
+        for b in range(NL // 2):
+            for k in range(2):
+                tg = a([t], lambda: S.activation(T.xg[0:32, 64 * b + k:64 * b + 64:2], T.xf[32 * b:32 * b + 32, 32 * k:32 * k + 32], COPY))
         yield
-        v([t], lambda: V.tensor_copy(T.xu[:, 0:64:2], T.xf[:, 0:32]))
+        t = v([tg], lambda: V.tensor_copy(T.offb[0:32, :], T.xg[0:32, :]))
         yield
-        t = v([], lambda: V.tensor_copy(T.xu[:, 1:64:2], T.xf[:, 32:64]))
-        for b in (3, 0, 1, 2):
-            for d in range(4):
-                t_ob[b] = dma("s", [t, ("cl0", cnt["cl0"])], T.offb[32 * d:32 * d + 32, 64 * b:64 * b + 64],
-                              T.xu[32 * b:32 * b + 32, :], "ob%d" % b)
+        t = v([t], lambda: V.tensor_copy(T.offb[32:64, :], T.offb[0:32, :]))
+        yield
+        t_ob.append(v([t], lambda: V.tensor_copy(T.offb[64:128, :], T.offb[0:64, :])))
         yield
     lists = big_lists()
+    fill = list(FILL)
 
-    banks = {"v": [T.ps0, T.ps1, T.ps2, T.ps3], "a": [T.ps4, T.ps5, T.ps6, T.ps7]}
-    hist = {"v": [], "a": []}
-    ready = {}
+    def gap():
+        for c in fill.pop(0):
+            if c == "L":
+                next(lists)
+            elif c != "-":
+                quant_w(int(c))
 
-    def product(s, h, o, e):
-        n = len(hist[e])
-        bank = banks[e][n % 4]
-        old = [hist[e][n - 4]] if n >= 4 else [t_own]
-        w0, c0 = 256 * h + 128 * o, CAP * SLOT[s]
-        tk = op("p", [t_c if s == r else ("c%d" % s, 2 * n_in[s])] + old + [t_wq[h // 2]], lambda: g.tensor.matmul_mx(
-            bank[:, 0:CAP], T.wq[:, w0:w0 + 128], T.wp[:, w0:w0 + 128], T.lq[:, c0:c0 + CAP], T.lp[:, c0:c0 + CAP],
-            True, True), "p" + e)
-        d0 = RW * (2 * h + o) + c0
+    def beats(out, s):
+        return tt([t_own, ("s%d" % s, n_in[s])], out[:], mine, T.sc[:, 32 * SLOT[s]:32 * SLOT[s] + 32], A.is_gt if s < r else A.is_ge)
+    beats(T.c1, senders[0])
+    t = beats(T.c2, senders[1])
+    t = tt([t], T.c12[:], T.c1[:], T.c2[:], A.mult)
+    t = beats(T.c3, senders[2])
+    gap()
+    t_win = tt([t], T.win[:], T.c12[:], T.c3[:], A.mult)
+    gap()
+    t1 = v([t_win, t_gc], lambda: V.tensor_tensor_scan(T.ra[0:96, :], T.m32[0:96, 0:32], T.win[0:96, :], 0.0, A.min, A.add))
+    b1 = tt([], T.w2[:], T.win[:], T.dl[:], A.mult)
+    gap()
+    t2 = v([t1], lambda: V.transpose(T.rt[0:96, 32:64], T.ra[0:96, :]))
+    b2 = tt([b1, t_dc], T.u2[:], T.dc[:], T.w2[:], A.subtract)
+    gap()
+    t3 = v([t2], lambda: V.tensor_tensor_scan(T.ea[0:96, :], T.rt[0:96, 31:63], T.lim[0:96, :], 0.0, A.add, A.min))
+    b3 = tt([b2], T.ta[:], T.u2[:], T.ra[:], A.add)
+    gap()
+    t4 = v([t3], lambda: V.transpose(T.et[0:96, :], T.ea[0:96, :]))
+    gap()
+    t6 = v([t4, b3], lambda: V.tensor_scalar(T.ou[:], T.ta[:], T.et[:, 31:32], 1.25, A.add, A.mult))
+    gap()
+    t7 = v([t6, t_vi, t_ll, t_vb], lambda: V.tensor_copy(T.ll[:].indirect(T.ou[:]), T.vi[:]))
+    gap()
+
+    def spread(e, b):
+        c0, shift = FIRST[b] * 5 // 4, float(XE - 4 * FIRST[b])
+        out, in_ = T.le[32 * b:32 * b + 32, :], T.ll[96:128, c0:c0 + 100]
         if e == "v":
-            c = v([tk], lambda: V.tensor_copy(T.rw[:, d0:d0 + CAP], bank[:, 0:CAP]))
-        else:
-            c = a([tk], lambda: S.activation(T.rw[:, d0:d0 + CAP], bank[:, 0:CAP], COPY))
-        hist[e].append(c)
-        ready[(s, h, o)] = c
+            return v([t7], lambda: V.tensor_scalar(out, in_, shift, None, A.add))
+        return a([t7], lambda: S.activation(out, in_, IDENT, bias=shift))
+    spread("a", 0)
+    spread("a", 1)
+    t8 = v([t7, t_kk], lambda: V.tensor_tensor_scan(T.sl5[:], T.ll[:, 0:240], T.kk[:], 8192.0, A.min, A.max))
+    gap()
+    t9 = v([t8], lambda: V.tensor_scalar(T.offa[:, 0:48], T.sl5[:, 4:240:5], t3f, None, A.add))
+    t10 = a([t9], lambda: S.activation(T.cb[:, 0:384], T.xb[:, 0:XE].indirect(T.offa[:, 0:24]), COPY))
+    spread("a", 2)
+    t_le = spread("a", 3)
+    gap()
+    t11 = v([t9], lambda: V.tensor_copy(T.cb[:, 384:768], T.xb[:, 0:XE].indirect(T.offa[:, 24:48])))
+    gap()
+    t_c = v([t10, t11], lambda: V.quantize_mx(T.lq[:, 3 * WID:3 * WID + CAP], T.lp[:, 3 * WID:3 * WID + CAP], T.cb[:, 0:4 * CAP]))
+    gap()
+    t_e = []
 
-    def add_dma(deps, out, in_, sem):
-        return op("g", deps, lambda: g.dma_start(out, in_, accum_op=A.add), sem, 16)
+    def further_columns():
+        t = v([t_le], lambda: V.tensor_tensor_scan(T.se[:], T.le[:], T.kk[:, 0:100], 8192.0, A.min, A.max))
+        yield
+        t = v([t], lambda: V.tensor_scalar(T.offa[:, 48:68], T.se[:, 4:100:5], t3f, float(XE + 4 * EX), A.add, A.min))
+        t = a([t, t_xe], lambda: S.activation(T.cb[:, 4 * CAP:4 * WID], T.xb[:].indirect(T.offa[:, 48:68]), COPY))
+        yield
+        c0 = 3 * WID + CAP
+        t_e.append(v([t, t_f3], lambda: V.quantize_mx(T.lq[:, c0:c0 + 128], T.lp[:, c0:c0 + 128], T.cb[:, 4 * CAP:4 * (CAP + 128)])))
+        yield
+    further = further_columns()
 
-    got = {}
-    cur = {}
-    left = [sum(1 for st in PLAN if st[0] == "s" and int(st[2]) == o and st[3:] != "h") for o in range(2)]
-    done = [0, 0]
-    extra = [int(st[1]) for st in PLAN if st[0] == "g" and st[1] != "7"]
+    def sends(n, ks):
+        need("g", t_e if n == 3 else [t_c])
+        if n == 4:
+            rid, pid, _se = topo.addr(relay_of(core))
+            m = feed_mask(core, peers[0])
+            g.remote_dma(views(3, 0, CAP)[1], views(3, 0, CAP)[1], T.sem["fed1"], T.sem["cl"], pid, rid, m)
+            cnt["cl"] = cnt.get("cl", 0) + bin(m).count("1")
+            return
+        if n == 3:
+            for k in ks:
+                js = [j for j in range(3) if (j, k) not in WIDE]
+                cnt["cl"] += send_all([peers[j] for j in js], [views(j, CAP, WID)[k] for j in js], views(3, CAP, WID)[k], "e%d" % r, "cl")
+            return
+        d = relay_of(core) if n == 3 else peers[n]
+        rid, pid, _se = topo.addr(d)
+        m = feed_mask(core, peers[0]) if n == 3 else topo.mask(core, d)
+        lo, hi = (CAP, WID) if n == 3 else (0, CAP)
+        for k in ks:
+            if (n, k) in WIDE:
+                need("g", t_e)
+                hi = WID
+            g.remote_dma(views(n, lo, hi)[k], views(3, lo, hi)[k], T.sem["fed%d" % k if n == 3 else "c%d" % r], T.sem["cl"], pid, rid, m)
+            cnt["cl"] = cnt.get("cl", 0) + bin(m).count("1")
+
+    def codes(k):
+        return t_c if k == 0 else ("c%d" % senders[k - 1], 2 * n_in[senders[k - 1]])
+
+    def extra(k):
+        return t_e[0] if k == 0 else ("e%d" % senders[k - 1], sum((k - 1, j) not in WIDE for j in range(2)) * n_in[senders[k - 1]])
+
+    def window(e, k, h, o, take):
+        c0 = WID * ((k - 1) % NR)
+        d0 = RW * (2 * h + o) + CAP * ((k - 1) % NR)
+        ready[(k, h, o)] = product((k, h, o), e, h, o, [([codes(k)], T.lq, T.lp, c0, c0 + CAP)],
+                                   (lambda tk, bank: copy(e, [tk], T.rw[:, d0:d0 + CAP], bank[:, 0:CAP])) if take else None)
+
+    first_bank = {}
+    nd = [0]
+
+    def add_dma(deps, out, in_):
+        nd[0] += 1
+        return op("g", deps, lambda: g.dma_start(out, in_, accum_op=A.add), "d%d" % nd[0], 16)
+
+    have = {n: [] for n in "abcdef01"}
+
+    def behind(n, c0, c1):
+        return [t for (p0, p1, t) in have[n] if p0 < c1 and c0 < p1]
+
+    def holds(n, c0, c1, t):
+        have[n].append((c0, c1, t))
+        return t
+
+    def from_psum(e, n, c0, c1, b0):
+        old, out = behind(n, c0, c1), T["ac" + n][:, c0:c1]
+        if old:
+            return lambda tk, bank: holds(n, c0, c1, tt([tk] + old, out, bank[:, b0:b0 + c1 - c0], out, A.add))
+        return lambda tk, bank: holds(n, c0, c1, copy(e, [tk], out, bank[:, b0:b0 + c1 - c0]))
     for step in PLAN:
+        take = step[0] != "+"
+        step, _, part = step.lstrip("+").partition("/")
+        c0, c1 = PARTS[part]
         if step == "L":
-            next(lists)
-        elif step == "Q":
-            quant_w(3)
+            next(lists, None)
+        elif step == "T":
+            next(further)
+        elif step == "N":
+            dma("g", t_wn, T.wn[:], T.wnt[:], "wn")
+        elif step[0] == "S":
+            sends(int(step[1]), [int(k) for k in step[2:] or "01"])
+        elif step[0] == "F":
+            need("g", [t_c])
+            k, js = int(step[1]), [int(c) for c in step[2:]]
+            cnt["cl"] = cnt.get("cl", 0) + send_all([peers[j] for j in js], [views(j, 0, CAP)[k] for j in js], views(3, 0, CAP)[k],
+                                                    "c%d" % r, "cl")
+        elif step[0] == "Q":
+            quant_w(int(step[1]))
+        elif step[0] == "*":
+            o = int(step[1])
+            if o not in first_bank:
+                first_bank[o] = len(hist["v"])
+                hist["v"] += [None] * 4
+            n0 = first_bank[o]
+            for k in (int(c) for c in step[2:]):
+                for j, b in enumerate(BORDER[o]):
+                    n, end, w0 = (WID if b == 3 else 128), WID * ((k - 1) % NR) + WID, wcol[("v", b)] + 128 * o
+                    bank = banks["v"][(n0 + j) % 4]
+                    need("p", [codes(k), extra(k), hist["v"][n0 + j - 4], t_wq[("v", b)]])
+                    call = lambda: g.tensor.matmul_mx(bank[:, 0:n], T.wq[:, w0:w0 + 128], T.wp[:, w0:w0 + 128], T.lq[:, end - n:end],
+                                                      T.lp[:, end - n:end], k == 0, k == NR - 1)
+                    if k < NR - 1:
+                        call()
+                    else:
+                        ahead["B%d%d" % (b, o)] = ("v", n0 + j, op("p", [], call, "pv"), bank)
+        elif step[1] == "B":
+            b, o = int(step[2]), int(step[3])
+            n, lo = (WID, 0) if b == 3 else (128, FIRST[b])
+            ends = [(k, WID * ((k - 1) % NR) + WID) for k in range(NR)]
+            product(step[1:4], step[0], ("v", b), o, [([codes(k), extra(k)], T.lq, T.lp, end - n, end) for k, end in ends],
+                    from_psum(step[0], step[4], lo, FIRST[b] + EX, n - (FIRST[b] + EX - lo)) if take else None)
         elif step[0] in "va":
-            product(([r] + senders)[int(step[1])], int(step[2]), int(step[3]), step[0])
+            window(step[0], int(step[1]), int(step[2]), int(step[3]), take)
+        elif step[0] in "YZ":
+            n, o = step[1:3]
+            old, out = behind(o, c0, c1), T.y[:, 512 * int(o) + c0:512 * int(o) + c1]
+            deps = behind(n, c0, c1) + old
+            if old:
+                t = add_dma(deps, out, T["ac" + n][:, c0:c1])
+            else:
+                nd[0] += 1
+                t = dma("s" if step[0] == "Y" else "a", deps, out, T["ac" + n][:, c0:c1], "d%d" % nd[0])
+            holds(o, c0, c1, t)
+        elif step[0] == "D":
+            n, m = step[1:3]
+            holds(n, c0, c1, add_dma(behind(n, c0, c1) + behind(m, c0, c1), T["ac" + n][:, c0:c1], T["ac" + m][:, c0:c1]))
         else:
-            h, o = int(step[1]), int(step[2])
-            halves = {"": (0, 1), "l": (0,), "h": (1,)}[step[3:]]
-            c0, c1 = 256 * halves[0], 256 * halves[-1] + 256
+            h, o, n = int(step[1]), int(step[2]), step[3]
             d0 = RW * (2 * h + o)
-            picked = T.rw[:, d0:d0 + RW].indirect(T.offb[:, 32 * h + c0 // 16:32 * h + c1 // 16])
-            deps = [ready[(s, h, o)] for s in range(NR)] + [t_ob[h // 2]]
-            if step[0] == "g":
-                out = T[GBUF[(h, o)]]
-                got[(h, o)] = a(deps, lambda: S.activation(out[:, c0:c1], picked, COPY))
-                if h == 7:
-                    for k in halves:
-                        cur[(o, k)] = (out, got[(h, o)])
-                elif h == extra[-1]:
-                    t_g = got[(h, 0)] if len(extra) == 1 else add_dma([got[(5, 0)], got[(6, 0)]], T.g6[:], T.g5[:], "ga")
-                continue
-            if step[3:] != "h":
-                done[o] += 1
-            out = T["ac%d" % (2 * o + done[o] % 2)]
-            tk = tt([cur[(o, k)][1] for k in halves] + deps, out[:, c0:c1], picked, cur[(o, halves[0])][0][:, c0:c1], A.add)
-            for k in halves:
-                cur[(o, k)] = (out, tk)
-            if done[o] == left[o] and o == 1:
-                dma(("s", "a")[halves[0]], [tk], T.y[:, 512 + c0:512 + c1], out[:, c0:c1], "y%d" % (1 + halves[0]))
-            elif done[o] == left[o] and halves != (0,):
-                t_y0 = dma("s", [tk], T.y[:, 0:512], out[:], "y0")
-                y0 = out
-    if extra:
-        add_dma([t_g, t_y0], T.y[:, 0:512], T.g6[:], "gb")
+            wide = RW if h < NE else NR * CAP
+            picked = T.rw[:, d0:d0 + wide].indirect(T.offb[:, 32 * h + c0 // 16:32 * h + c1 // 16])
+            deps = [ready[(k, h, o)] for k in range(NR)] + t_ob
+            old, out = behind(n, c0, c1), T["ac" + n][:, c0:c1]
+            if old:
+                holds(n, c0, c1, tt(deps + old, out, picked, out, A.add))
+            else:
+                holds(n, c0, c1, copy("a" if step[0] == "g" else "v", deps, out, picked))
 
     need("g", sorted(cnt.items()))

from concourse.bass import DstId, RemoteDMATransfer
from concourse.mybir import dt, AluOpType, ActivationFunctionType

CAP = 192
NR = 4
NL = 6
NE = 4
EX = 80
WID = CAP + EX
XE = 4 * 576
OWN = 3 * CAP
RW = OWN + 512
LW = 6016
SLOT = (0, 2, 1, 3)
F, I32, U16, BF, X4, U8 = "float32", "int32", "uint16", "bfloat16", "float8_e4m3fn_x4", "uint8"
_sb = {
    "us_sb": (32, BF), "ut": (4 * 142, BF), "uq": (142, X4), "up": (142, U8), "sh": (64, F),
    "xb": (XE + 4 * EX + 16, BF), "xq": (576, X4), "xp": (576, U8),
    "zt": (512, BF), "wm": (7 * 1024, BF), "wq": (2560, X4), "wp": (2560, U8),
    "cb": (4 * (CAP + 128), BF), "lq": (3 * WID + CAP + 128, X4), "lp": (3 * WID + CAP + 128, U8), "sc": (128, F),
    "pre": (192, F), "col": (192, F), "ia": (32, F),
    "vi": (512, F), "vt": (512, F), "dl": (32, F), "dc": (32, F), "ki": (240, F), "kk": (240, F), "m32": (128, F), "lim": (32, F),
    "c1": (32, F), "c2": (32, F), "c3": (32, F), "c12": (32, F), "win": (32, F), "ra": (32, F), "rt": (64, F), "ea": (32, F),
    "et": (32, F), "w2": (32, F), "u2": (32, F), "ta": (32, F), "ou": (32, U16), "ll": (LW, F), "sl5": (240, F),
    "offa": (WID // 4, U16), "le": (100, F), "se": (100, F),
    "ab": (128, F), "m64": (64, F), "cc": (64, F), "ww": (128, F), "rr": (1024, F), "rt4": (64, F), "e4": (32, F), "et4": (32, F),
    "p4": (128, F), "pm": (128, F), "ph": (64, F), "dd": (64, F), "xf": (64, F), "xg": (32 * NL, F), "offb": (32 * NL, U16),
    "q1": (32, F), "q2": (32, F), "wnt": (32, F),
    "rw": (2 * NL * RW, F), "aca": (512, F), "acb": (512, F), "acc": (512, F), "acd": (512, F), "ace": (512, F), "acf": (512, F),
}
SCRATCH = {k: ("sbuf", [128, n], d) for k, (n, d) in _sb.items()}
for _k in range(8):
    SCRATCH["ps%d" % _k] = ("psum", [128, 512], F)
SEMAPHORES = (["v", "a", "pv", "pa", "px", "pb", "gi", "us", "xe", "zd", "wn", "sloc", "cl", "fed0", "fed1"]
              + [n + str(i) for n in ("x", "s", "c", "e") for i in range(4)]
              + ["w%d" % i for i in range(7)] + ["d%d" % i for i in range(1, 11)])

BLK = {0: 1, 2: 2, 4: 3, 5: 4, 1: 5, 3: 6}
VBLK = {3: 0, 0: 1, 1: 2, 2: 3}
QUANT = ((0, 2), (1, 3), (4, 5))
FIRST = {3: CAP, 0: CAP + EX, 1: CAP + 2 * EX, 2: CAP + 3 * EX}
XLOAD = ((2, 4), (1, 2), (0, 1))
RELAY = ()
EARLY = "00 01 20 21 10 11 30 31".split()
FILL = "LL LL L L LL L LL LL L LL LL -".split()
WIDE = ()
BORDER = ((1, 2, 0, 3), (3, 0, 1, 2))
GS = 40
PARTS = {"": (0, 512), "l": (0, 352), "h": (352, 512), "x": (0, 256), "y": (256, 512)}
PLAN = """
S0 S1 S2 T L L T Q3 L a040 a041 v050 L Q4 L T S310 a051 Q5 Q6
a150 v100 a140 v110 L a130 v120 L a151 v101 L N a111 v121
a250 v200 a240 v210 a230 v220 a251 v201
v300 a350 v310 a340 v320 s00a/y s00a/x g50c +a330 +a351 +a301 *00 g40d Dcd s10a/y s10a/x a330 a351 a301 +a211 +a311
*0123 s20a/y s20a/x g51b/l g51b/h s30a/y s30a/x vB10a vB20a vB00a vB30a Ya0 Yc0 a211 a311 a221 a321 *101
s01b/l s01b/h a131 a231 a331 *12 s11b/l s11b/h a141 a241 a341 *13
s21b/l s21b/h s31b/l s31b/h vB31b vB01b vB11b vB21b s41b/l Yb1/l s41b/h Zb1/h
""".split()


def rank_program(g, core, T, topo):
    r = T.rank_of(core)

    def relay_of(c):
        return [k for k in topo.cores_of(c) if topo.die(k) == topo.die(c) and T.rank_of(k) is None][0]

    def views(n, lo, hi):
        return T.lq[:, WID * n + lo:WID * n + hi].bitcast(dt.uint8), T.lp[:, WID * n + lo:WID * n + hi]

    def send_all(ds, outs, view, rsem, lsem):
        ids = [DstId(rid=topo.addr(d)[0], pnc=topo.addr(d)[1]) for d in ds]
        g.remote_dma_fused([RemoteDMATransfer(dst_ids=ids, dma_engine_mask=topo.mask(core, ds[0]), remote_sem=T.sem[rsem],
                                              srcs=[view], dsts=outs)], local_sem=T.sem[lsem])
        return len(topo.engines(core, ds[0]))

    def feed_mask(c, far):
        return topo.mask(c, relay_of(c)) & ~topo.mask(c, far)
    if r is None:
        for s, c in enumerate(T.cores):
            if RELAY and relay_of(c) == core:
                ds = [T.cores[(s + 1 + n) % NR] for n in RELAY]
                g.wait_ge(T.sem["fed1"], bin(feed_mask(c, ds[0])).count("1"))
                g.wait_ge(T.sem["cl"], send_all(ds, [views(n, 0, CAP)[1] for n in RELAY], views(3, 0, CAP)[1], "c%d" % s, "cl"))
        return
    A = AluOpType
    COPY = ActivationFunctionType.Copy
    IDENT = ActivationFunctionType.Identity
    Q = {"g": g, "v": g.vector, "a": g.scalar, "p": g.tensor, "s": g.sync}
    seen = {k: {} for k in Q}
    cnt = {}

    def need(qn, deps):
        for s, n in deps:
            if seen[qn].get(s, 0) < n:
                Q[qn].wait_ge(T.sem[s], n)
                seen[qn][s] = n

    def op(qn, deps, call, sem, n=1):
        need(qn, deps)
        call().then_inc(T.sem[sem], n)
        cnt[sem] = cnt.get(sem, 0) + n
        return (sem, cnt[sem])

    V = g.vector
    S = g.scalar

    def v(deps, call):
        return op("v", deps, call, "v")

    def a(deps, call):
        return op("a", deps, call, "a")

    def dma(qn, deps, out, in_, sem):
        return op(qn, deps, lambda: Q[qn].dma_start(out, in_), sem, 16)

    def tt(deps, out, in0, in1, alu):
        return v(deps, lambda: V.tensor_tensor(out, in0, in1, alu))

    peers = [T.cores[(r + k) % NR] for k in (1, 2, 3)]
    senders = [(r - k) % NR for k in (1, 2, 3)]
    u = SLOT[r]

    t_us = dma("s", [], T.us_sb[:], T.us[:, 0:32], "us")
    t_x = {}
    for n, (lo, hi) in enumerate(XLOAD):
        t = dma("s", [], T.xb[:, 512 * lo:512 * hi], T.x[:, 512 * lo:512 * hi], "x%d" % n)
        t_x.update({i: t for i in range(lo, hi)})

    def io(out, pattern, base, cm):
        return op("g", [], lambda: g.iota(out, pattern, base, cm, allow_small_or_imprecise_dtypes=True), "gi")
    io(T.pre[:, 0:32], [[0, 8], [1, 4]], 0, 0)
    io(T.pre[:, 32:64], [[0, 2], [1, 4], [0, 4]], 0, 0)
    io(T.pre[:, 64:96], [[0, 2], [-2048, 4], [0, 4]], 0, 0)
    io(T.pre[:, 96:128], [[0, 2], [32, 16]], 0, 0)
    io(T.pre[:, 128:160], [[0, 16], [-1, 2]], 1, 0)
    t_pre = io(T.pre[:, 160:192], [[0, 16], [1, 2]], 0, 0)
    t3f, alf = T.col[:, 0:1], T.col[:, 32:33]
    t_ki = io(T.ki[:], [[0, 48], [1, 5]], -1, 0)
    io(T.ia[:], [[1, 32]], 1, 0)
    t_dl = io(T.dl[:], [[1, 32]], 200, 32)
    t_vi = io(T.vi[:], [[4, 32], [128, 16]], 0, 0)

    t_zt = v([], lambda: V.memset(T.zt[:], 0.0))
    t_u0 = v([], lambda: V.memset(T.ut[:], 0.0))
    t_f = v([], lambda: V.memset(T.xb[:, 2048:XE], 0.0))
    v([], lambda: V.memset(T.et[96:128, 31:32], 0.0))
    v([], lambda: V.memset(T.rt[:, 0:32], 0.0))
    v([], lambda: V.memset(T.rt4[:, 0:32], 0.0))
    t_f2 = v([], lambda: V.memset(T.rr[:, 159:1024:32], 0.0))
    v([], lambda: V.memset(T.xb[:, XE + 4 * EX:XE + 4 * EX + 16], 0.0))
    t_f3 = v([], lambda: V.memset(T.cb[:, 4 * WID:4 * (CAP + 128)], 0.0))
    t_z = {}

    def zero_a(b, ks=(0, 1)):
        for k in ks:
            c0 = 1024 * b + 512 * k
            t_z[b] = a([t_zt], lambda: S.activation(T.wm[:, c0:c0 + 512], T.zt[:], COPY))

    def zero_v(b, k=None):
        c0, n = (1024 * b, 1024) if k is None else (1024 * b + 512 * k, 512)
        t_z[b] = v([], lambda: V.memset(T.wm[:, c0:c0 + n], 0.0))

    def quant_x(i):
        lo, hi = 128 * i, (576 if i == 3 else 128 * i + 128)
        return v([t_x[i], t_f], lambda: V.quantize_mx(T.xq[:, lo:hi], T.xp[:, lo:hi], T.xb[:, 4 * lo:4 * hi]))
    zero_a(BLK[2], (0,))
    for k in range(2):
        c0 = 1024 * BLK[5] + 512 * k
        t_z[BLK[5]] = dma("s", [t_zt], T.wm[:, c0:c0 + 512], T.zt[:], "zd")

    for e in range(4):
        b0, b1 = 4 * 14 + e, 4 * 15 + e
        t_ua = a([t_us, t_u0], lambda: S.activation(T.ut[:, b1:b1 + 449:64], T.us_sb[:, e:32:4], COPY))
        t_ut = v([t_us, t_u0], lambda: V.tensor_copy(T.ut[:, b0:b0 + 449:64], T.us_sb[:, e:32:4]))
    zero_a(BLK[2], (1,))
    zero_v(BLK[0], 0)
    t_uq = v([t_ut, t_ua], lambda: V.quantize_mx(T.uq[:], T.up[:], T.ut[:]))
    for i in (3, 2, 1, 0):
        t_q = quant_x(i)
        if i == 2:
            zero_v(BLK[0], 1)
        need("p", [t_uq, t_q])
        if i == 1:
            t_col = v([t_pre], lambda: V.transpose(T.col[:], T.pre[:]))
        for k in (2 * i + 1, 2 * i):
            st = 14 - 2 * k
            call = lambda: g.tensor.matmul_mx(T.ps0[:, 0:128], T.uq[:, st:st + 128], T.up[:, st:st + 128],
                                              T.xq[:, 64 * k:64 * k + 128], T.xp[:, 64 * k:64 * k + 128], k == 7, k == 0)
            if k:
                call()
            else:
                t_sm = op("p", [], call, "px")
    zero_v(BLK[4], 0)
    mine = T.sc[:, 32 * u:32 * u + 32]
    t = tt([t_sm, t_col], T.sh[:], T.ps0[:, 0:64], T.col[:, 128:192], A.mult)
    zero_v(BLK[4], 1)
    t_own = tt([t], mine, T.sh[:, 0:32], T.sh[:, 32:64], A.add)
    need("g", [t_own])
    t_sent = ("sloc", send_all(peers, [mine] * 3, mine, "s%d" % r, "sloc"))
    cnt["sloc"] = t_sent[1]
    n_in = {s: len(topo.engines(T.cores[s], core)) for s in senders}
    t_vt = io(T.vt[:], [[16, 8], [4 + 2048, 4], [128, 16]], 0, 0)
    io(T.lim[:], [[0, 2], [4096, 16]], 0, 0)
    t_gc = io(T.m32[:], [[0, 4], [4096, 32]], 0, 0)
    t_ll = io(T.ll[:, 0:640], [[0, 640]], 2048, 0)

    zero_a(BLK[1])
    zero_a(BLK[3])
    t_w = {}
    t_wq = {}
    wcol = {}

    def load_w(i):
        for h in QUANT[i]:
            c0 = 1024 * BLK[h]
            t_w[i] = dma("s", [t_z[BLK[h]]], T.wm[16 * h:16 * h + 16, c0:c0 + 1024], T.w[16 * h:16 * h + 16, :], "w%d" % i)

    def load_v(b, deps):
        c0, i = 1024 * VBLK[b], 3 + VBLK[b]
        t_w[i] = dma("s", deps, T.wm[32 * b:32 * b + 32, c0:c0 + 1024], T.w[96:128, :], "w%d" % i)

    def quant_w(i):
        keys = QUANT[i] if i < 3 else [("v", b) for b in VBLK if VBLK[b] == i - 3]
        c0, q0, n = (1024 * BLK[keys[0]], 512 * i, 512) if i < 3 else (1024 * (i - 3), 768 + 256 * i, 256)
        t = v([t_w[i]], lambda: V.quantize_mx(T.wq[:, q0:q0 + n], T.wp[:, q0:q0 + n], T.wm[:, c0:c0 + 4 * n]))
        for j, k in enumerate(keys):
            t_wq[k] = t
            wcol[k] = q0 + 256 * j
    load_w(0)
    load_w(1)
    load_w(2)
    quant_w(0)
    for b in FIRST:
        t_xe = dma("s", [t_sent], T.xb[32 * b:32 * b + 32, XE:XE + 4 * EX], T.x[96:128, 4 * FIRST[b]:4 * FIRST[b] + 4 * EX], "xe")
    t_kk = v([t_col, t_ki], lambda: V.tensor_scalar(T.kk[:], T.ki[:], alf, 8192.0, A.is_lt, A.mult))
    v([t_dl], lambda: V.tensor_scalar(T.ra[96:128, :], T.ia[96:128, :], T.col[96:128, 96:97], None, A.add))
    if NE:
        v([], lambda: V.tensor_scalar(T.p4[0:16 * NE, 32 * u:32 * u + 32], T.ia[0:16 * NE, :], T.col[0:16 * NE, 96:97], OWN - 1.0,
                                      A.add, A.add))
    quant_w(1)
    quant_w(2)
    t_dc = a([t_dl], lambda: S.activation(T.dc[:], T.dl[:], IDENT, bias=-0.5))

    banks = {"v": [T.ps0, T.ps1, T.ps2, T.ps3], "a": [T.ps4, T.ps5, T.ps6, T.ps7]}
    hist = {"v": [], "a": []}
    ready = {}

    def copy(e, deps, out, in_):
        if e == "v":
            return v(deps, lambda: V.tensor_copy(out, in_))
        return a(deps, lambda: S.activation(out, in_, COPY))

    ahead = {}

    def product(name, e, key, o, moving, out):
        if name in ahead:
            e, n, tk, bank = ahead.pop(name)
            hist[e][n] = out(tk, bank)
            return hist[e][n]
        n = len(hist[e])
        bank = banks[e][n % 4]
        old = [hist[e][n - 4]] if n >= 4 else [t_own]
        w0 = wcol[key] + 128 * o
        for i, (deps, q, p, c0, c1) in enumerate(moving):
            need("p", deps + old + [t_wq[key]])
            call = lambda: g.tensor.matmul_mx(bank[:, 0:c1 - c0], T.wq[:, w0:w0 + 128], T.wp[:, w0:w0 + 128], q[:, c0:c1], p[:, c0:c1],
                                              i == 0, i == len(moving) - 1)
            if i < len(moving) - 1:
                call()
            else:
                tk = op("p", [], call, "p" + e)
        if out is None:
            ahead[name] = (e, n, tk, bank)
        hist[e].append(out and out(tk, bank))
        return hist[e][n]

    def early(job):
        h, o = int(job[0]), int(job[1])
        d0 = RW * (2 * h + o) + OWN
        ready[(0, h, o)] = product(job, "a", h, o, [([t_q], T.xq, T.xp, 0, 512)],
                                   lambda tk, bank: copy("a", [tk], T.rw[:, d0:d0 + 512], bank[:]))
    zero_a(VBLK[3])
    load_v(3, [t_z[VBLK[3]]])
    for b in range(3):
        load_v(b, [t_wq[2 * b]])
    for job in EARLY[:2]:
        early(job)
    t_vb = a([t_vt, t_vi, t_col], lambda: S.activation(T.vi[96:128, :], T.vt[96:128, :], IDENT, bias=T.col[96:128, 64:65]))
    for job in EARLY[2:]:
        early(job)

    t_ob = []
    t_wn = []
    lo64, hi64 = T.sc[:, 0:64], T.sc[:, 64:128]

    def column(deps, s):
        c0, p0 = 32 * SLOT[s], (16 * NE if s == r else 0)
        base = OWN if s == r else CAP * senders.index(s)
        return v(deps, lambda: V.tensor_scalar(T.p4[p0:128, c0:c0 + 32], T.rr[p0:128, c0:c0 + 32], T.et4[p0:128, SLOT[s]:SLOT[s] + 1],
                                               float(base - 1), A.add, A.add))

    def big_lists():
        m1 = tt([], T.m64[:], lo64, hi64, A.max)
        yield
        tt([], T.ab[:, 64:128], hi64, lo64, A.is_gt)
        yield
        tt([m1], T.cc[:, 0:32], T.m64[:, 32:64], T.m64[:, 0:32], A.is_le)
        yield
        t = tt([], T.cc[:, 32:64], T.m64[:, 32:64], T.m64[:, 0:32], A.is_gt)
        yield
        m2 = tt([], T.ab[:, 0:64], hi64, lo64, A.is_le)
        yield
        w1 = tt([t], T.ww[:, 64:128], T.ab[:, 64:128], T.cc[:], A.mult)
        yield
        m3 = tt([m2], T.ww[:, 0:64], T.ab[:, 0:64], T.cc[:], A.mult)
        yield
        q1 = tt([w1], T.q1[:], T.ww[:, 64:96], T.ww[:, 96:128], A.add)
        yield
        n1 = v([m3], lambda: V.tensor_tensor_scan(T.rr[:, 0:128], T.m32[:], T.ww[:], 0.0, A.min, A.add))
        yield
        q2 = tt([q1], T.q2[:], T.q1[:], T.cc[:, 32:64], A.add)
        yield
        t = v([n1, t_f2], lambda: V.transpose(T.rt4[:, 32:64], T.rr[:, 31:1024:32]))
        yield
        t_wn.append(tt([q2], T.wnt[:], T.q2[:], T.cc[:, 32:64], A.add))
        yield
        t = v([t], lambda: V.tensor_tensor_scan(T.e4[:], T.rt4[:, 31:63], T.lim[:], 0.0, A.add, A.min))
        yield
        n4 = v([t], lambda: V.transpose(T.et4[:], T.e4[:]))
        yield
        for s in range(NR):
            p4 = column([n4], s)
            yield
        for k in range(2):
            t = tt([p4], T.pm[:, 64 * k:64 * k + 64], T.p4[:, 64 * k:64 * k + 64], T.ww[:, 64 * k:64 * k + 64], A.mult)
            yield
        t = tt([t], T.ph[:], T.pm[:, 0:64], T.pm[:, 64:128], A.add)
        yield
        for k in range(4):
            c = 16 * (k // 2)
            td = tt([t], T.dd[:, 16 * k:16 * k + 16], T.ph[:, c:c + 16], T.ph[:, 32 + c:48 + c], A.add)
        yield
        t = v([td], lambda: V.transpose(T.xf[:], T.dd[:]))
        for b in range(NL // 2):
            for k in range(2):
                tg = a([t], lambda: S.activation(T.xg[0:32, 64 * b + k:64 * b + 64:2], T.xf[32 * b:32 * b + 32, 32 * k:32 * k + 32], COPY))
        yield
        t = v([tg], lambda: V.tensor_copy(T.offb[0:32, :], T.xg[0:32, :]))
        yield
        t = v([t], lambda: V.tensor_copy(T.offb[32:64, :], T.offb[0:32, :]))
        yield
        t_ob.append(v([t], lambda: V.tensor_copy(T.offb[64:128, :], T.offb[0:64, :])))
        yield
    lists = big_lists()
    fill = list(FILL)

    def gap():
        for c in fill.pop(0):
            if c == "L":
                next(lists)
            elif c != "-":
                quant_w(int(c))

    def beats(out, s):
        return tt([t_own, ("s%d" % s, n_in[s])], out[:], mine, T.sc[:, 32 * SLOT[s]:32 * SLOT[s] + 32], A.is_gt if s < r else A.is_ge)
    beats(T.c1, senders[0])
    t = beats(T.c2, senders[1])
    t = tt([t], T.c12[:], T.c1[:], T.c2[:], A.mult)
    t = beats(T.c3, senders[2])
    gap()
    t_win = tt([t], T.win[:], T.c12[:], T.c3[:], A.mult)
    gap()
    t1 = v([t_win, t_gc], lambda: V.tensor_tensor_scan(T.ra[0:96, :], T.m32[0:96, 0:32], T.win[0:96, :], 0.0, A.min, A.add))
    b1 = tt([], T.w2[:], T.win[:], T.dl[:], A.mult)
    gap()
    t2 = v([t1], lambda: V.transpose(T.rt[0:96, 32:64], T.ra[0:96, :]))
    b2 = tt([b1, t_dc], T.u2[:], T.dc[:], T.w2[:], A.subtract)
    gap()
    t3 = v([t2], lambda: V.tensor_tensor_scan(T.ea[0:96, :], T.rt[0:96, 31:63], T.lim[0:96, :], 0.0, A.add, A.min))
    b3 = tt([b2], T.ta[:], T.u2[:], T.ra[:], A.add)
    gap()
    t4 = v([t3], lambda: V.transpose(T.et[0:96, :], T.ea[0:96, :]))
    gap()
    t6 = v([t4, b3], lambda: V.tensor_scalar(T.ou[:], T.ta[:], T.et[:, 31:32], 1.25, A.add, A.mult))
    gap()
    t7 = v([t6, t_vi, t_ll, t_vb], lambda: V.tensor_copy(T.ll[:].indirect(T.ou[:]), T.vi[:]))
    gap()

    def spread(e, b):
        c0, shift = FIRST[b] * 5 // 4, float(XE - 4 * FIRST[b])
        out, in_ = T.le[32 * b:32 * b + 32, :], T.ll[96:128, c0:c0 + 100]
        if e == "v":
            return v([t7], lambda: V.tensor_scalar(out, in_, shift, None, A.add))
        return a([t7], lambda: S.activation(out, in_, IDENT, bias=shift))
    spread("a", 0)
    spread("a", 1)
    t8 = v([t7, t_kk], lambda: V.tensor_tensor_scan(T.sl5[:], T.ll[:, 0:240], T.kk[:], 8192.0, A.min, A.max))
    gap()
    t9 = v([t8], lambda: V.tensor_scalar(T.offa[:, 0:48], T.sl5[:, 4:240:5], t3f, None, A.add))
    t10 = a([t9], lambda: S.activation(T.cb[:, 0:384], T.xb[:, 0:XE].indirect(T.offa[:, 0:24]), COPY))
    spread("a", 2)
    t_le = spread("a", 3)
    gap()
    t11 = v([t9], lambda: V.tensor_copy(T.cb[:, 384:768], T.xb[:, 0:XE].indirect(T.offa[:, 24:48])))
    gap()
    t_c = v([t10, t11], lambda: V.quantize_mx(T.lq[:, 3 * WID:3 * WID + CAP], T.lp[:, 3 * WID:3 * WID + CAP], T.cb[:, 0:4 * CAP]))
    gap()
    t_e = []

    def further_columns():
        t = v([t_le], lambda: V.tensor_tensor_scan(T.se[:], T.le[:], T.kk[:, 0:100], 8192.0, A.min, A.max))
        yield
        t = v([t], lambda: V.tensor_scalar(T.offa[:, 48:68], T.se[:, 4:100:5], t3f, float(XE + 4 * EX), A.add, A.min))
        t = a([t, t_xe], lambda: S.activation(T.cb[:, 4 * CAP:4 * WID], T.xb[:].indirect(T.offa[:, 48:68]), COPY))
        yield
        c0 = 3 * WID + CAP
        t_e.append(v([t, t_f3], lambda: V.quantize_mx(T.lq[:, c0:c0 + 128], T.lp[:, c0:c0 + 128], T.cb[:, 4 * CAP:4 * (CAP + 128)])))
        yield
    further = further_columns()

    def sends(n, ks):
        need("g", t_e if n == 3 else [t_c])
        if n == 4:
            rid, pid, _se = topo.addr(relay_of(core))
            m = feed_mask(core, peers[0])
            g.remote_dma(views(3, 0, CAP)[1], views(3, 0, CAP)[1], T.sem["fed1"], T.sem["cl"], pid, rid, m)
            cnt["cl"] = cnt.get("cl", 0) + bin(m).count("1")
            return
        if n == 3:
            for k in ks:
                js = [j for j in range(3) if (j, k) not in WIDE]
                cnt["cl"] += send_all([peers[j] for j in js], [views(j, CAP, WID)[k] for j in js], views(3, CAP, WID)[k], "e%d" % r, "cl")
            return
        d = relay_of(core) if n == 3 else peers[n]
        rid, pid, _se = topo.addr(d)
        m = feed_mask(core, peers[0]) if n == 3 else topo.mask(core, d)
        lo, hi = (CAP, WID) if n == 3 else (0, CAP)
        for k in ks:
            if (n, k) in WIDE:
                need("g", t_e)
                hi = WID
            g.remote_dma(views(n, lo, hi)[k], views(3, lo, hi)[k], T.sem["fed%d" % k if n == 3 else "c%d" % r], T.sem["cl"], pid, rid, m)
            cnt["cl"] = cnt.get("cl", 0) + bin(m).count("1")

    def codes(k):
        return t_c if k == 0 else ("c%d" % senders[k - 1], 2 * n_in[senders[k - 1]])

    def extra(k):
        return t_e[0] if k == 0 else ("e%d" % senders[k - 1], sum((k - 1, j) not in WIDE for j in range(2)) * n_in[senders[k - 1]])

    def window(e, k, h, o, take):
        c0 = WID * ((k - 1) % NR)
        d0 = RW * (2 * h + o) + CAP * ((k - 1) % NR)
        ready[(k, h, o)] = product((k, h, o), e, h, o, [([codes(k)], T.lq, T.lp, c0, c0 + CAP)],
                                   (lambda tk, bank: copy(e, [tk], T.rw[:, d0:d0 + CAP], bank[:, 0:CAP])) if take else None)

    first_bank = {}
    nd = [0]

    def add_dma(deps, out, in_):
        nd[0] += 1
        return op("g", deps, lambda: g.dma_start(out, in_, accum_op=A.add), "d%d" % nd[0], 16)

    have = {n: [] for n in "abcdef01"}

    def behind(n, c0, c1):
        return [t for (p0, p1, t) in have[n] if p0 < c1 and c0 < p1]

    def holds(n, c0, c1, t):
        have[n].append((c0, c1, t))
        return t

    def from_psum(e, n, c0, c1, b0):
        old, out = behind(n, c0, c1), T["ac" + n][:, c0:c1]
        if old:
            return lambda tk, bank: holds(n, c0, c1, tt([tk] + old, out, bank[:, b0:b0 + c1 - c0], out, A.add))
        return lambda tk, bank: holds(n, c0, c1, copy(e, [tk], out, bank[:, b0:b0 + c1 - c0]))
    for step in PLAN:
        take = step[0] != "+"
        step, _, part = step.lstrip("+").partition("/")
        c0, c1 = PARTS[part]
        if step == "L":
            next(lists, None)
        elif step == "T":
            next(further)
        elif step == "N":
            dma("g", t_wn, T.wn[:], T.wnt[:], "wn")
        elif step[0] == "S":
            sends(int(step[1]), [int(k) for k in step[2:] or "01"])
        elif step[0] == "F":
            need("g", [t_c])
            k, js = int(step[1]), [int(c) for c in step[2:]]
            cnt["cl"] = cnt.get("cl", 0) + send_all([peers[j] for j in js], [views(j, 0, CAP)[k] for j in js], views(3, 0, CAP)[k],
                                                    "c%d" % r, "cl")
        elif step[0] == "Q":
            quant_w(int(step[1]))
        elif step[0] == "*":
            o = int(step[1])
            if o not in first_bank:
                first_bank[o] = len(hist["v"])
                hist["v"] += [None] * 4
            n0 = first_bank[o]
            for k in (int(c) for c in step[2:]):
                for j, b in enumerate(BORDER[o]):
                    n, end, w0 = (WID if b == 3 else 128), WID * ((k - 1) % NR) + WID, wcol[("v", b)] + 128 * o
                    bank = banks["v"][(n0 + j) % 4]
                    need("p", [codes(k), extra(k), hist["v"][n0 + j - 4], t_wq[("v", b)]])
                    call = lambda: g.tensor.matmul_mx(bank[:, 0:n], T.wq[:, w0:w0 + 128], T.wp[:, w0:w0 + 128], T.lq[:, end - n:end],
                                                      T.lp[:, end - n:end], k == 0, k == NR - 1)
                    if k < NR - 1:
                        call()
                    else:
                        ahead["B%d%d" % (b, o)] = ("v", n0 + j, op("p", [], call, "pv"), bank)
        elif step[1] == "B":
            b, o = int(step[2]), int(step[3])
            n, lo = (WID, 0) if b == 3 else (128, FIRST[b])
            ends = [(k, WID * ((k - 1) % NR) + WID) for k in range(NR)]
            product(step[1:4], step[0], ("v", b), o, [([codes(k), extra(k)], T.lq, T.lp, end - n, end) for k, end in ends],
                    from_psum(step[0], step[4], lo, FIRST[b] + EX, n - (FIRST[b] + EX - lo)) if take else None)
        elif step[0] in "va":
            window(step[0], int(step[1]), int(step[2]), int(step[3]), take)
        elif step[0] in "YZ":
            n, o = step[1:3]
            old, out = behind(o, c0, c1), T.y[:, 512 * int(o) + c0:512 * int(o) + c1]
            deps = behind(n, c0, c1) + old
            if old:
                t = add_dma(deps, out, T["ac" + n][:, c0:c1])
            else:
                nd[0] += 1
                t = dma("s" if step[0] == "Y" else "a", deps, out, T["ac" + n][:, c0:c1], "d%d" % nd[0])
            holds(o, c0, c1, t)
        elif step[0] == "D":
            n, m = step[1:3]
            holds(n, c0, c1, add_dma(behind(n, c0, c1) + behind(m, c0, c1), T["ac" + n][:, c0:c1], T["ac" + m][:, c0:c1]))
        else:
            h, o, n = int(step[1]), int(step[2]), step[3]
            d0 = RW * (2 * h + o)
            wide = RW if h < NE else NR * CAP
            picked = T.rw[:, d0:d0 + wide].indirect(T.offb[:, 32 * h + c0 // 16:32 * h + c1 // 16])
            deps = [ready[(k, h, o)] for k in range(NR)] + t_ob
            old, out = behind(n, c0, c1), T["ac" + n][:, c0:c1]
            if old:
                holds(n, c0, c1, tt(deps + old, out, picked, out, A.add))
            else:
                holds(n, c0, c1, copy("a" if step[0] == "g" else "v", deps, out, picked))

    need("g", sorted(cnt.items()))
